import numpy as np, ml_dtypes
CORES = [40,41,42,43,44,45,46,47]
N = 8
BF = ml_dtypes.bfloat16
P, CB, W, RU, HB = 3072, 12, 4096, 3, 3
def step(x, inv, wa, kc, hi, lo):
    v = np.add.reduce(x * wa[..., None], axis=2); src = v >= hi[..., None]; blk = v <= lo[..., None]
    cl = np.add.reduce((x >= 128) * kc[..., None], axis=2)
    new = []
    for a in range(N):
        b = max(0, a - HB); L = (a - b + 1) * P; at = np.arange(L)
        s = np.concatenate(src[b:a + 1], axis=1); k = np.concatenate(cl[b:a + 1], axis=1)
        wall = np.maximum.accumulate(np.where(np.concatenate(blk[b:a + 1], axis=1), at, -1), axis=1)[:, L - P:]
        near = np.full((8, P), -1)
        for c in range(16):
            last = np.maximum.accumulate(np.where(s & (k == c), at, -1), axis=1)
            last = np.concatenate([np.full((8, 1), -1), last[:, :-1]], axis=1)[:, L - P:]
            near = np.where(cl[a] == c, last, near)
        ok = (near > wall) & ~blk[a]
        got = np.take_along_axis(np.concatenate(x[b:a + 1], axis=2), np.maximum(near, 0)[:, None, :], 2)
        new.append(np.where(ok[:, None, :] & (x[a] < 64), got, x[a]))
    x = np.stack(new)
    code = np.add.reduce((x[:, :, :CB] >= 128) * (1 << np.arange(CB))[:, None], axis=2)
    return (x + np.take_along_axis(inv, code[:, :, None, :], 3)) & 255
def parts(rng):
    x = rng.integers(0, 256, (N, 8, 16, P)); few = rng.choice(np.array([0.0, 0.2, 0.4]), (N, 8, 1, 1))
    x = np.where(rng.random(x.shape) < few, x >> 2, x); inv = rng.integers(0, 256, (N, 8, 16, W))
    wa = rng.integers(-3, 4, (N, 8, 16, RU)); wa[:, :, 0] = rng.choice(np.array([-3, -2, 2, 3]), (N, 8, RU))
    o = np.argsort(rng.random((N, 8, 16, RU)), axis=2); kc = np.where(o < 4, 1 << np.minimum(o, 3), 0)
    m = 127.5 * np.sum(wa, axis=2); s = 74.0 * np.sqrt(np.sum(wa * wa, axis=2))
    hi = np.floor(m + s * rng.choice(np.array([0.5, 1.0, 1.5, 3.0]), (N, 8, RU))).astype(np.int64)
    lo = np.floor(m - s * rng.choice(np.array([1.5, 2.0, 2.5, 9.0]), (N, 8, RU))).astype(np.int64)
    return x, inv, wa, kc, hi, lo
def pack(x, inv, wa, kc, hi, lo):
    return {"x": x.reshape(N, 128, P).astype(np.float32).astype(BF), "inv": inv.reshape(N, 128, W).astype(np.float32).astype(BF),
            "wa": wa.reshape(N, 128, RU).astype(np.float32).astype(BF), "kc": kc.reshape(N, 128, RU).astype(np.float32).astype(BF),
            "hl": np.repeat(np.concatenate([hi, lo], axis=2), 16, axis=1).astype(np.float32)}
def fit(x, inv, wa, kc, qh, ql):
    hi = np.zeros((N, 8, RU), np.int64); lo = np.zeros((N, 8, RU), np.int64)
    ih = (qh * (P - 1)).astype(np.int64)[..., None]; il = np.maximum(ql * (P - 1), 0).astype(np.int64)[..., None]
    for u in range(RU):
        v = np.sort(np.add.reduce(x * wa[..., u][..., None], axis=2), axis=-1)
        hi[..., u] = np.take_along_axis(v, ih, -1)[..., 0]
        lo[..., u] = np.minimum(np.where(ql < 0, v[..., 0] - 1, np.take_along_axis(v, il, -1)[..., 0]), hi[..., u] - 1)
        x = step(x, inv, wa[..., u], kc[..., u], hi[..., u], lo[..., u])
    return hi, lo
def staged(rng, x, inv, wa, kc, hi, lo, kind, kl):
    wa[..., 0] = 0; wa[:, :, 15, 0] = 3; kc[..., 0] = 0; hi[..., 0] = 738; lo[..., 0] = 27
    x[:, :, 15] = np.where(kind == 1, rng.integers(246, 256, kind.shape), np.where(kind == 2, rng.integers(0, 10, kind.shape), rng.integers(10, 246, kind.shape)))
    for i, w in enumerate((1, 6, 11, 14)):
        kc[:, :, w, 0] = 1 << i; x[:, :, w] = (x[:, :, w] & 127) + 128 * ((kl >> i) & 1)
    return pack(x, inv, wa, kc, hi, lo)
def setup_inputs(rng):
    return pack(*parts(rng))
def setup_inputs_full(rng):
    p = parts(rng); r = rng.random((N, 8, P)); kind = np.where(r < 0.05, 1, np.where(r < 0.055, 2, 0)); kl = rng.integers(0, 16, (N, 8, P))
    x, hi, lo = p[0], p[4], p[5]
    for q in range(N):
        for g in range(8):
            e = P - 16 - int(rng.integers(0, 48)); mode = g % 5 if q == 0 else int(rng.integers(0, 5))
            if mode == 2:
                kind[q, g] = np.where(kind[q, g] == 2, 0, kind[q, g]); kl[q, g] = np.where(kind[q, g] == 1, rng.integers(0, 16), kl[q, g])
            else:
                kind[q, g, e:] = 0; kind[q, g, e:e + 16] = 1; kl[q, g, e:e + 16] = rng.permutation(16)
                if mode == 1: kind[q, g, P - 1] = 2
                if mode == 3: kind[q, g, e - 1] = 2
                if mode == 4: kind[q, g, e + 8] = 2
            kind[q, g, :P // 2 if q == 1 else int(rng.choice(np.array([0, 1, 40, P // 2])))] = 0
    c = rng.permutation(16)
    kind[0, 2] = np.where(rng.random(P) < 0.97, 1, 0); kl[0, 2] = np.where(kind[0, 2] == 1, c[2], kl[0, 2])
    kind[:HB + 1, 7] = 1; kl[:HB + 1, 7] = c[0]; kl[0, 7, 1] = c[1]
    kind[HB, 7, P - 32:] = 0; kl[HB, 7, P - 32:] = c[1]
    x[:HB + 1, 7, 2:4] = x[:HB + 1, 7, 2:4] >> 2; x[HB, 7, 0, P - 32:] = x[HB, 7, 0, P - 32:] >> 2; x[0, 7, 0, 1] = 200
    hi[:2, 0, 1] = 16384; lo[:2, 0, 1] = -16384
    return staged(rng, *p, kind, kl)
def setup_inputs_ends(rng):
    p = parts(rng); kind = np.zeros((N, 8, P), np.int64); kl = rng.integers(0, 16, (N, 8, P)); some = (rng.random((N, 8, P)) < 0.05).astype(np.int64)
    g, h, j = rng.permutation(8)[:3]
    for q in range(N):
        o = np.concatenate([np.array([g]), rng.permutation(np.delete(np.arange(8), g))])
        kind[q, o[1], 0] = 1; kind[q, o[2], P - 1] = 1
        kind[q, o[3]] = some[q, o[3]]; kind[q, o[3], 0] = 2
        kind[q, o[4]] = 1; kind[q, o[5]] = 2
        kind[q, o[6], ::2] = 1; kind[q, o[6], 1::2] = 2
        kind[q, o[7]] = some[q, o[7]]; kind[q, o[7], P - 2] = 1; kind[q, o[7], P - 1] = 2
    kind[:, g] = 0; kind[0, g] = some[0, g]
    kind[:2, h] = 0; kind[0, h, 0] = 1; kind[:2, j] = 0; kind[0, j, P - 1] = 1
    return staged(rng, *p, kind, kl)
def setup_inputs_ties(rng):
    x, inv, wa, kc, hi, lo = parts(rng)
    x = np.where(rng.random(x.shape) < 0.5, rng.choice(np.array([0, 63, 64, 127, 128, 255]), x.shape), x)
    inv = np.where(rng.random(inv.shape) < 0.5, rng.choice(np.array([0, 1, 64, 128, 192, 255]), inv.shape), inv)
    ql = rng.choice(np.array([0.0, 0.03, 0.1, 0.85]), (N, 8)); ql[0, 0] = 0.85; ql[1, 0] = 0.03
    for g, w in ((2, 3), (3, -3)):
        wa[:, g, :, 0] = w; ql[:, g] = 0.03
        small = (kc[:, g, :, 0] == 0)[..., None] & (rng.random((N, 16, P)) < 0.15)
        x[:, g] = np.where(rng.random((N, 1, P)) < 0.2, 255, np.where(small, 0, 192) + (x[:, g] >> 2))
    hi, lo = fit(x, inv, wa, kc, np.full((N, 8), 0.85), ql)
    return pack(x, inv, wa, kc, hi, lo)
def setup_inputs_alike(rng):
    x, inv, wa, kc, hi, lo = parts(rng)
    pat = rng.choice(np.array([0, 63, 64, 128, 255]), (N, 8, 16, 6)); pat[..., 0] = 0; pat[..., 1] = 255; pat[:, :, 0, 2] = 64; pat[:, :, 1, 2] = 128
    x = np.take_along_axis(pat, rng.integers(0, 6, (N, 8, 1, P)), 3); inv[:, 1::2] = 0
    hi, lo = fit(x, inv, wa, kc, np.full((N, 8), 0.6), rng.choice(np.array([-1.0, 0.05]), (N, 8)))
    return pack(x, inv, wa, kc, hi, lo)
def setup_inputs_spread(rng):
    x, inv, wa, kc, hi, lo = parts(rng)
    x = np.floor(np.exp2(8 * rng.random((N, 8, 1, P))) * rng.random((N, 8, 16, P))).astype(np.int64)
    inv = np.where(rng.random((N, 8, 1, W)) < 0.5, np.floor(np.exp2(8 * rng.random((N, 8, 1, W))) * rng.random((N, 8, 16, W))).astype(np.int64), inv)
    wa = np.where(rng.random(wa.shape) < 0.6, 0, rng.choice(np.array([-3, -1, 1, 3]), wa.shape))
    hi, lo = fit(x, inv, wa, kc, rng.choice(np.array([0.5, 0.9, 0.99, 0.9995]), (N, 8)), rng.choice(np.array([-1.0, 0.0, 0.01, 0.1]), (N, 8)))
    return pack(x, inv, wa, kc, hi, lo)
def check_inputs(d):
    bad = []
    for k, lo, hi in (("x", 0, 255), ("inv", 0, 255), ("wa", -3, 3), ("kc", 0, 8), ("hl", -16384, 16384)):
        a = np.asarray(d[k]).astype(np.float32)
        if not np.all((a >= lo) & (a <= hi) & (a == np.floor(a))): bad.append("range of " + k)
    k = np.sort(np.asarray(d["kc"]).astype(np.float32).reshape(N, 8, 16, RU), axis=2)
    if not np.all(k == np.array([0] * 12 + [1, 2, 4, 8], np.float32)[:, None]): bad.append("class weights of kc")
    h = np.asarray(d["hl"]).astype(np.float32).reshape(N, 8, 16, 2 * RU)
    if not np.all(h == h[:, :, :1]): bad.append("rows of hl alike in a group")
    if not np.all(h[..., RU:] < h[..., :RU]): bad.append("lo under hi")
    return bad
def reference(x, inv, wa, kc, hl):
    z = x.astype(np.float32).astype(np.int32).reshape(N, 8, 16, P); tab = inv.astype(np.float32).astype(np.int32).reshape(N, 8, 16, W)
    w = wa.astype(np.float32).astype(np.int32).reshape(N, 8, 16, RU); k = kc.astype(np.float32).astype(np.int32).reshape(N, 8, 16, RU)
    h = hl.astype(np.int32).reshape(N, 8, 16, 2 * RU)[:, :, 0]
    for u in range(RU): z = step(z, tab, w[..., u], k[..., u], h[..., u], h[..., RU + u])
    return {"y": z.reshape(N, 128, P).astype(np.float32).astype(BF)}

@@ -1,0 +1,421 @@
+from concourse.bass import DstId, RemoteDMATransfer
+from concourse.mybir import AluOpType as ALU, ActivationFunctionType as ACT, AxisListType as AX
+
+P, W0, RU, HB, TW = 3072, 32, 3, 3, 4096
+CH = [512, 1024, 1024, 512]
+CD = [512, 1024, 1536]
+BIT = ["vvvv", "aavv", "aavv"]
+LOW = ["vvvv", "vvaa", "vvaa"]
+STEP = ["aaav", "aaav", "aaav"]
+BND = ["aaaa", "aaaa", "aaaa"]
+INV = ["avvv", "avvv", "aavv"]
+FLR = ["aaaa", "aaaa", "aaaa"]
+U, KF, KN = 2.0 ** -9, 24576.0, 49152.0
+ENG_PER_DST, GP = 4, 512
+CYC, PCY, LAT_X, LAT_S, GATH, XCH = 1.04, 0.52, 180.0, 90.0, 1.56, 3200.0
+ORDER = "IIiIhdhNhLhShMhMhMhLhLEGEDDBAAaAAZRKBTRAATMOQHAATRKChELXhBhKhHhOCaASELhKaGiahQBCdhDhDFcFZffaahIhAdJhHDiAHiOXZchChAaaeadGiAhdKhVFJWYIXhNFhVhThNRRARQEPPBOBNhHhBCBhDIDAbLLPJKOXLAILLQRKIIHIQDPGOANFMHTLSSHFHIIFMWXMHHHHIGJHINMHJKHFRFGZFVXFiRHMHFWKYXPUPTIJFMFGFFAHEGHHEEIIIFHhNHHFEhGLFSHHHHHEhDEFFhAEEEEEVYHMIFGEEHEBDLNAROLKJFDLHCALBKBJJEBHRHHNBGBBEBHUBGBBENONEWBDUBJBXBBGCNBECDQOOBNUBTDLODNBEBBJBBEBFFBHCBhRCAFAMCCABBEGEEBfcAbCCCAAEaaAAAADBQPYYSHWOSAAAEEABHHAAHBJJJAIAHQHCPOOEAAAABBHBBUFFQRAPbFOOYOPOEIADAFAOBHBGCJJJEIFCGEABDBAA"
+
+
+def _scratch():
+    s = {}
+
+    def add(names, n, dt):
+        for x in names.split():
+            s[x] = ("sbuf", [128, n], dt)
+    for u in range(RU):
+        add("xw%d" % u, W0 + P, "bfloat16")
+        add("ws%d wka%d wkv%d" % (u, u, u), 144, "bfloat16")
+        add("mma%d mmv%d" % (u, u), 128, "bfloat16")
+        add("oh%d" % u, 512, "bfloat16")
+        add("summ%d" % u, 16, "int32")
+        add("land%d" % u, 48, "int32")
+    add("bt d0 lo fb nb yo ig", P, "bfloat16")
+    add("sel rr ss", P, "float16")
+    add("dd", P + 16, "float16")
+    add("bb", P, "float32")
+    add("tab", TW, "bfloat16")
+    add("fl", 1536, "bfloat16")
+    add("offk offi offc", 192, "uint16")
+    add("offs", 2, "uint16")
+    add("t1 t2 k16", 192, "bfloat16")
+    add("lc", 192, "float16")
+    add("jr", 144, "float32")
+    add("gr gma gmv", 128, "float32")
+    add("pat", 640, "bfloat16")
+    add("id1 id16 ida idv id4k", 128, "bfloat16")
+    add("idh id2", 128, "float16")
+    add("en", 144, "float16")
+    add("pf pla plv em", 144, "bfloat16")
+    add("step", 48, "bfloat16")
+    add("pi", 4, "int32")
+    add("col q16 thr wkf hls", 16, "float32")
+    add("was kcs", 8, "bfloat16")
+    add("cmb", 48, "int32")
+    for b in range(8):
+        s["ps%d" % b] = ("psum", [128, 512], "float32")
+    return s
+
+
+SCRATCH = _scratch()
+SEMAPHORES = ["ev", "ea", "ep", "eg", "loc", "st", "arr0", "arr1", "arr2"] + ["dm%d" % i for i in range(12)]
+ENGSEM = {"v": "ev", "a": "ea", "p": "ep", "g": "eg"}
+
+
+def _cuts(sizes):
+    return [(sum(sizes[:i]), sum(sizes[:i + 1])) for i in range(len(sizes))]
+
+
+def _pieces(a, b, m=512):
+    n = (b - a + m - 1) // m
+    return [(a + i * (b - a) // n, a + (i + 1) * (b - a) // n) for i in range(n)]
+
+
+def _program(g, T, topo, rank):
+    ops, hist, at, nd = [], {}, ["c0", 0, 0], [0]
+    V, A, PE = g.vector, g.scalar, g.tensor
+
+    def stage(name, u=0, n=0):
+        at[0], at[1], at[2] = name, n, u
+
+    def op(eng, cost, fn, rd=(), wr=(), tok=None, soft=(), dma=None, lat=0.0, pre=None):
+        i = len(ops)
+        deps = set()
+        for (lst, is_w) in ((rd, False), (wr, True)):
+            for (b, lo, hi) in lst:
+                deps |= {j for (j, l2, h2, w2) in hist.get(b, ()) if (is_w or w2) and l2 < hi and lo < h2}
+        for (lst, is_w) in ((rd, False), (wr, True)):
+            for (b, lo, hi) in lst:
+                h = hist.setdefault(b, [])
+                if is_w:
+                    h[:] = [e for e in h if not (lo <= e[1] and e[2] <= hi)]
+                h.append((i, lo, hi, is_w))
+        if tok is not None:
+            deps |= {j for j in tok["ops"] if ops[j]["e"] != eng}
+            soft = list(soft) + tok["ops"][-1:]
+            tok["ops"].append(i)
+        deps.discard(i)
+        ops.append({"e": eng, "c": cost, "fn": fn, "deps": deps, "soft": set(soft) - deps, "tok": tok, "dma": dma, "lat": lat,
+                    "pre": pre, "key": "%s.%d" % (at[0], at[1]), "u": at[2]})
+        at[1] += 1
+        return i
+
+    def token(kind):
+        return {"kind": kind, "ops": [], "b": None}
+
+    def ap(x):
+        if not isinstance(x, tuple):
+            return x
+        if len(x) == 2:
+            return T["ps%d" % x[0]["b"]][:, 0:x[1]]
+        if len(x) == 6:
+            return T[x[0]][:, x[1]:x[2]].indirect(T[x[3]][:, x[4]:x[5]])
+        return T[x[0]][:, x[1]:x[2]]
+
+    def call(eng, f, fn, out, args, tail=(), kw=None, **k):
+        rd, tok = [], None
+        for x in list(args) + list((kw or {}).values()):
+            if isinstance(x, tuple):
+                if len(x) == 2:
+                    tok = x[0]
+                else:
+                    rd += [x[0:3]] + ([x[3:6]] if len(x) == 6 else [])
+        cost = max(64.0, (out[2] - out[1]) * f) * CYC + (30.0 if eng == "v" else 60.0)
+        return op(eng, cost, lambda: fn(ap(out), *[ap(x) for x in args], *tail, **{q: ap(x) for q, x in (kw or {}).items()}),
+                  rd, [out], tok=tok, **k)
+
+    def ts(out, in0, s1, o0, s2=None, o1=None, f=1.0, **k):
+        return call("v", f, V.tensor_scalar, out, [in0, s1, s2], [o0] if o1 is None else [o0, o1], **k)
+
+    def tt(out, in0, in1, o, f=1.0, **k):
+        return call("v", f, V.tensor_tensor, out, [in0, in1], [o], **k)
+
+    def act(out, in_, func, f=1.0, **kw):
+        return call("a", f, A.activation, out, [in_], [func], kw)
+
+    def mset(out, val):
+        return call("v", 0.5, V.memset, out, [val])
+
+    def mm(tok, n, items, start=True, stop=True, **k):
+        rd, cnt = [], 0
+        for it in items:
+            rd += [it[0], it[1]] if len(it) == 2 else [(it[0], 0, 144), it[1:]]
+            cnt += 1 if len(it) == 2 else 16
+
+        def fn():
+            prs = []
+            for it in items:
+                prs += [(ap(it[0]), ap(it[1]))] if len(it) == 2 else [
+                    (T[it[0]][:, 15 - i:143 - i], T[it[1]][:, it[2] + i:it[3]:16]) for i in range(16)]
+            for q, (lhs, rhs) in enumerate(prs):
+                last = PE.matmul(ap((tok, n)), lhs, rhs, start and q == 0, stop and q == len(prs) - 1)
+            return last
+        return op("p", cnt * max(64, n) * PCY + 20.0, fn, rd, (), tok=tok, **k)
+
+    def iota(out, pattern, base, cm, **kw):
+        return op("g", 160.0 + 2 * CYC * (out[2] - out[1]), lambda: g.iota(ap(out), pattern, base, cm, **kw), (), [out])
+
+    def dma(eng, out, in_, rd, wr, nbytes, sem=None):
+        if sem is None:
+            sem = "dm%d" % nd[0]
+            nd[0] += 1
+        q = g.sync if eng == "s" else g.scalar
+        return op(eng, 60.0, lambda: q.dma_start(out, in_), rd, wr, dma=sem, lat=1900.0 + nbytes / 300.0)
+
+    def col(i, b="col"):
+        return (b, i, i + 1)
+
+    def whole(b):
+        return (b, 0, 128)
+
+    ch, small = _cuts(CH), {"allow_small_or_imprecise_dtypes": True}
+    add, mul, eq = ALU.add, ALU.mult, ALU.is_equal
+    dma("a", T.kcs[:, 0:3], T.kc[:, :], (), [("kcs", 0, 8)], 0)
+    dma("a", T.was[:, 0:3], T.wa[:, :], (), [("was", 0, 8)], 0)
+    dma("a", T.hls[:, 0:6], T.hl[:, :], (), [("hls", 0, 8)], 0)
+    for (a, b) in ch:
+        dma("s", T.xw0[:, W0 + a:W0 + b], T.x[:, a:b], (), [("xw0", W0 + a, W0 + b)], b * 256)
+    dma("s", T.tab[:, :], T.inv[:, :], (), [("tab", 0, TW)], (P + TW) * 256)
+
+    jr, kc3 = ("jr", 0, 144), ("kcs", 0, 3)
+    iota(("pi", 0, 1), [[0, 1]], 0, 1)
+    iota(jr, [[1, 144]], 0, 0, **small)
+    ts(("pi", 1, 2), ("pi", 0, 1), 15, ALU.bitwise_and)
+    call("v", 1.0, V.tensor_copy, ("col", 0, 2), [("pi", 0, 2)])
+    ts(col(3), col(0), col(1), ALU.subtract)
+    ts(col(2), col(0), col(1), ALU.subtract, 15.0, add)
+    ts(("em", 0, 144), jr, col(2), eq)
+    act(("wkf", 0, 3), ("was", 0, 3), ACT.Identity)
+    act(("wkf", 4, 7), kc3, ACT.Identity)
+    act(("wkf", 8, 11), kc3, ACT.Identity, scale=2.0)
+    ts(("thr", 0, 3), kc3, 0.0, eq, 0.75, ALU.subtract)
+    ts(("thr", 12, 15), kc3, 1.0, ALU.min, 128.0, mul)
+    act(("thr", 4, 7), ("hls", 3, 6), ACT.Identity, scale=-1.0, bias=-0.5)
+    act(("thr", 8, 11), ("hls", 0, 3), ACT.Identity, scale=-1.0, bias=0.5)
+    ts(whole("id1"), whole("jr"), col(0), eq)
+    for (b, v) in (("id16", 16.0), ("ida", 256.0), ("idv", 512.0), ("id4k", 4096.0)):
+        act(whole(b), whole("id1"), ACT.Identity, scale=v)
+    ts(whole("idh"), whole("id1"), 1.0, mul, f=0.5)
+    ts(whole("id2"), whole("id1"), 2.0, mul, f=0.5)
+    ts(col(4), col(1), 16.0, add)
+    ts(col(5), col(1), -U, mul, (15 - 2048) * U, add)
+    ts(col(6), col(1), float(W0 - 1 - 2048 - 49 * 2048 - 4096), add)
+    ts(("dd", 0, 1), col(1), -U, mul, (15 - 2048) * U, add)
+    mset(("step", 0, 16), 8.0)
+    ts(("step", 16, 48), ("jr", 0, 32), col(4), eq, -65536.0, mul)
+    ts(("step", 16, 48), ("step", 16, 48), U, add)
+    mset(("fl", 0, max(CH)), -4.0)
+    ts(("en", 0, 144), ("em", 0, 144), -512.0, mul, f=0.5)
+    ts(("q16", 0, 16), ("jr", 0, 16), col(1), ALU.is_lt, 1.0, add)
+    call("v", 1.0, V.tensor_reduce, col(7), [("q16", 0, 16)], [AX.X, mul])
+    ts(col(8), col(1), 12.0, ALU.is_lt)
+    ts(col(9), col(7), col(8), mul, 1.0 / 128, mul)
+    act(("pf", 0, 144), ("em", 0, 144), ACT.Identity, scale=col(9))
+    act(("pla", 0, 144), ("pf", 0, 144), ACT.Identity, scale=-64.0)
+    act(("plv", 0, 144), ("pf", 0, 144), ACT.Identity, scale=-128.0)
+    iota(whole("gr"), [[16, 8], [0, 16]], 0, 0, **small)
+    for b in range(4):
+        iota(("pat", 128 * b, 128 * b + 128), [[0, 64 >> b], [8, 2], [0, 1 << b]], -3, 0, **small)
+    iota(("pat", 512, 640), [[0, 128]], -1, 0, **small)
+    iota(("k16", 0, 192), [[16, 192]], 0, 0, **small)
+    ts(whole("gma"), whole("gr"), col(3), eq)
+    act(whole("gmv"), whole("gma"), ACT.Identity, scale=2.0)
+    for u in range(RU):
+        stage("M%d" % u)
+        iota(("xw%d" % u, 0, 32), [[-15872, 2], [0, 16]], -512, 0, **small)
+        act(("ws%d" % u, 0, 144), ("em", 0, 144), ACT.Identity, scale=col(u, "wkf"))
+        tk = token("m")
+        oh = [("oh%d" % u, 128 * b, 128 * b + 128) for b in range(4)]
+        for b in range(4):
+            ts(oh[b], whole("id1"), col(4 + u, "wkf"), mul, float(1 << b), eq, 0.5)
+        mm(tk, 128, [(oh[b], ("pat", 128 * b, 128 * b + 128)) for b in range(4)] + [(whole("id1"), ("pat", 512, 640))])
+        for e in sorted(set(BIT[u])):
+            act(("wk%s%d" % (e, u), 0, 144), ("em", 0, 144), ACT.Identity, scale=col((4 if e == "a" else 8) + u, "wkf"))
+            tt(whole("mm%s%d" % (e, u)), (tk, 128), whole("gm" + e), mul)
+
+    def rule(u):
+        xw = "xw%d" % u
+        for j, (a, b) in enumerate(ch):
+            stage("A%d" % j, u)
+            ka, kb, n = a // 16, b // 16, (b - a) // 16
+            t_s, t_k = token("s"), token("k")
+            mm(t_s, n, [("ws%d" % u, xw, W0 + a, W0 + b)])
+            act(("t1", ka, kb), (t_s, n), ACT.Sign, bias=col(4 + u, "thr"))
+            act(("t2", ka, kb), (t_s, n), ACT.Sign, bias=col(8 + u, "thr"))
+            if BIT[u][j] == "v":
+                ts(("bt", a, b), (xw, W0 + a, W0 + b), col(12 + u, "thr"), ALU.is_ge, 0.5, ALU.subtract, 0.5)
+            else:
+                for (pa, pb) in _pieces(a, b):
+                    act(("bt", pa, pb), (xw, W0 + pa, W0 + pb), ACT.Sign, bias=col(u, "thr"), scale=1.0 / 170)
+            stage("A%d" % j, u, 10)
+            mm(t_k, n, [("wk%s%d" % (BIT[u][j], u), "bt", a, b)], True, False)
+            mm(t_k, n, [(whole("id16"), ("t1", ka, kb)), (whole("id16"), ("t2", ka, kb))], False, True)
+            ts(("offk", ka, kb), (t_k, n), 0.5, mul, 23.5, add)
+            src = ("step", 0, 48, "offk", ka, kb)
+            if STEP[u][j] == "a":
+                act(("d0", a, b), src, ACT.Identity, GATH)
+            else:
+                call("v", GATH, V.tensor_copy, ("d0", a, b), [src])
+            sent = call("v", 0.5, V.tensor_tensor_scan, ("dd", a + 1, b + 1), [("d0", a, b), ("fl", 0, b - a), ("dd", a, a + 1) if a else col(5)],
+                        [add, ALU.max])
+        stage("S0", u)
+        dsts = [rank + d for d in range(1, HB + 1) if rank + d < len(T.cores)]
+        if dsts:
+            sm = ("summ%d" % u, 0, 16)
+            ts(("offs", 0, 1), ("dd", P, P + 1), -512.0, mul, float(P - 1 + W0 - 2048), add)
+            ts(sm, (xw, 0, W0 + P, "offs", 0, 1), float(512 + 1024 * (rank + 1)), add, 0.0, ALU.max)
+
+            def send():
+                trs = []
+                for q, r2 in enumerate(dsts):
+                    rid, pid = topo.addr(T.cores[r2])[:2]
+                    eng = topo.engines(T.cores[rank], T.cores[r2])[q * ENG_PER_DST:(q + 1) * ENG_PER_DST]
+                    trs.append(RemoteDMATransfer(dst_ids=[DstId(rid=rid, pnc=pid)], dma_engine_mask=sum(1 << e for e in eng),
+                                                 remote_sem=T.sem["arr%d" % u], src=ap(sm), dst=ap(("land%d" % u, 16 * q, 16 * q + 16))))
+                g.remote_dma_fused(trs, local_sem=T.sem.loc)
+            sent = op("g", 1000.0, send, [sm], (), lat=XCH - 1000.0)
+        for j, (a, b) in enumerate(ch):
+            stage("D%d" % j, u)
+            for (pa, pb) in _pieces(a, b):
+                tk = token("mm")
+                mm(tk, pb - pa, [(whole("mm%s%d" % (BIT[u][j], u)), ("bt", pa, pb))], soft=[e[0] for e in hist["d0"] if e[1] < pb and pa < e[2]])
+                tt(("sel", pa, pb), ("dd", pa, pb), (tk, pb - pa), ALU.min)
+        for j, (a, b) in enumerate(_cuts(CD)):
+            stage("I%d" % j, u)
+            ka, kb, tk = a // 16, b // 16, token("i")
+            mm(tk, kb - ka, [(whole("id1"), ("k16", ka, kb)), (whole("id4k"), ("t1", ka, kb)), ("en", "sel", a, b)])
+            ts(("offi", ka, kb), (tk, kb - ka), col(6), add, 0.0, ALU.max)
+        for j, (a, b) in enumerate(ch):
+            stage("L%d" % j, u)
+            ka, kb, e = a // 16, b // 16, LOW[u][j]
+            for (pa, pb) in _pieces(a, b):
+                xs, tk = (xw, W0 + pa, W0 + pb), token("b")
+                if e == "a":
+                    act(("lo", pa, pb), xs, ACT.Sign, bias=-63.5)
+                else:
+                    ts(("lo", pa, pb), xs, 64.0, ALU.is_ge, 0.5, ALU.subtract, 0.5)
+                mm(tk, pb - pa, [(whole("id1"), xs), (whole("id" + e), ("lo", pa, pb))])
+                if BND[u][j] == "a":
+                    act(("bb", pa, pb), (tk, pb - pa), ACT.Identity)
+                else:
+                    call("v", 1.0, V.tensor_copy, ("bb", pa, pb), [(tk, pb - pa)])
+            if j % 2:
+                a = ch[j - 1][0]
+                tk = token("b")
+                mm(tk, (b - a) // 16, [("pl" + e, "lo", a, b)])
+                ts(("lc", a // 16, kb), (tk, (b - a) // 16), 0.5, add)
+        stage("R0", u)
+        ns = min(rank, HB)
+        if ns:
+            pre, src = ("arr%d" % u, ENG_PER_DST * ns), ("land%d" % u, 0, 16)
+            for q in range(1, ns):
+                dst = ("cmb", 16 * q - 16, 16 * q)
+                tt(dst, src, ("land%d" % u, 16 * q, 16 * q + 16), ALU.max, soft=[sent], pre=pre)
+                src, pre = dst, None
+            ts(("cmb", 32, 48), src, 1023, ALU.bitwise_and, soft=[sent], pre=pre)
+            ts((xw, 16, 32), ("cmb", 32, 48), -512.0, add)
+        nx, no = ("yo", 0) if u == RU - 1 else ("xw%d" % (u + 1), W0)
+        for j, (a, b) in enumerate(ch):
+            stage("B%d" % j, u)
+            ka, kb, tk = a // 16, b // 16, token("c")
+            for (pa, pb) in _pieces(a, b, GP):
+                tt(("rr", pa, pb), (xw, 0, W0 + P, "offi", pa // 16, pb // 16), ("bb", pa, pb), ALU.max, GATH, soft=[sent])
+                ts(("fb", pa, pb), ("rr", pa, pb), 0.0, ALU.max, KF - 63.5, add, 0.5)
+            mm(tk, kb - ka, [(whole("id2"), ("lc", ka, kb)), ("pf", "fb", a, b)])
+            ts(("offc", ka, kb), (tk, kb - ka), -(KF / 128 + 1) * 4095 - 1, add)
+            stage("B%d" % j, u, 10)
+            for (pa, pb) in _pieces(a, b, GP):
+                src = ("tab", 0, TW, "offc", pa // 16, pb // 16)
+                if INV[u][j] == "v":
+                    tt(("ss", pa, pb), src, ("rr", pa, pb), add, GATH)
+                    ts(("nb", pa, pb), ("ss", pa, pb), -1.0, mul, 127.5 - KN, add, 0.5)
+                else:
+                    act(("ig", pa, pb), src, ACT.Identity, GATH)
+            stage("B%d" % j, u, 20)
+            for (pa, pb) in _pieces(a, b):
+                tk, w = token("x"), pb - pa
+                if INV[u][j] == "v":
+                    mm(tk, w, [(whole("idh"), ("ss", pa, pb)), (whole("id1"), ("nb", pa, pb))])
+                else:
+                    both = [(whole("idh"), ("rr", pa, pb)), (whole("id1"), ("ig", pa, pb))]
+                    mm(tk, w, both)
+                    if FLR[u][j] == "a":
+                        act(("nb", pa, pb), (tk, w), ACT.Identity, scale=-1.0, bias=127.5 - KN)
+                    else:
+                        ts(("nb", pa, pb), (tk, w), -1.0, mul, 127.5 - KN, add)
+                    tk = token("x")
+                    mm(tk, w, both + [(whole("id1"), ("nb", pa, pb))])
+                act((nx, no + pa, no + pb), (tk, w), ACT.Identity, bias=KN)
+                if u == RU - 1:
+                    dma("s", T.y[:, pa:pb], T.yo[:, pa:pb], [("yo", pa, pb)], (), w * 256, sem="st")
+
+    for u in range(RU):
+        rule(u)
+    return ops
+
+
+def _arrange(ops, ref):
+    rest, pos, h = list(range(len(ref))), {}, 0
+    for s in ORDER:
+        if s > "f":
+            h = ord(s) - ord("g")
+        else:
+            i = rest.pop(32 * h + (ord(s) - ord("A") if s < "a" else ord(s) - ord("a") + 26))
+            pos[ref[i]["key"], ref[i]["u"]] = len(pos)
+            h = 0
+    at = []
+    for o in ops:
+        at.append(max([pos[o["key"], o["u"]]] + [at[d] + 1e-3 for d in o["deps"] | o["soft"]]))
+    loads = [i for i, o in enumerate(ops) if o["e"] == "s" and o["dma"] != "st"]
+    for i, p in zip(loads, sorted(at[i] for i in loads)):
+        at[i] = p - 1000
+    order = sorted(range(len(ops)), key=lambda i: (at[i], i))
+    fin, free, banks = {}, {}, [None] * 8
+    for i in order:
+        o = ops[i]
+        t = max([free.get(o["e"], 0.0)] + [fin[d] + (LAT_X if ops[d]["e"] != o["e"] or ops[d]["dma"] else LAT_S * (d in o["deps"]))
+                                          for d in o["deps"] | o["soft"]])
+        tok = o["tok"]
+        if tok is not None and tok["b"] is None:
+            f, tok["b"] = min((max(fin[j] for j in k["ops"]) + LAT_X if k else 0.0, b) for b, k in enumerate(banks)
+                              if not k or all(j in fin for j in k["ops"]))
+            if banks[tok["b"]]:
+                o["deps"] |= {j for j in banks[tok["b"]]["ops"] if ops[j]["e"] != "p"}
+            banks[tok["b"]], t = tok, max(t, f)
+        free[o["e"]] = t + o["c"]
+        fin[i] = t + o["c"] + o["lat"]
+    return order, max(fin.values())
+
+
+def rank_program(g, core, T, topo):
+    rank = T.rank_of(core)
+    if rank is None:
+        return
+    ops = _program(g, T, topo, rank)
+    order = _arrange(ops, _program(g, T, topo, HB))[0]
+    queue = {"v": g.vector, "a": g.scalar, "p": g.tensor, "g": g, "s": g.sync}
+    needed = set().union(*[o["deps"] for o in ops])
+    mark, total, clock, known = {}, {}, {}, {e: {} for e in queue}
+    place = {i: p for p, i in enumerate(order)}
+    for i in order:
+        o = ops[i]
+        q, kn = queue[o["e"]], known[o["e"]]
+        for d in sorted(o["deps"], key=lambda d: -place[d]):
+            s, v = mark[d]
+            if kn.get(s, 0) < v:
+                q.wait_ge(T.sem[s], v)
+                kn[s] = v
+                for s2, v2 in clock[d].items():
+                    kn[s2] = max(kn.get(s2, 0), v2)
+        if o["pre"] is not None:
+            q.wait_ge(T.sem[o["pre"][0]], o["pre"][1])
+        ins = o["fn"]()
+        if o["dma"] or i in needed:
+            s = o["dma"] or ENGSEM[o["e"]]
+            total[s] = total.get(s, 0) + (16 if o["dma"] else 1)
+            mark[i], clock[i] = (s, total[s]), dict(kn)
+            ins.then_inc(T.sem[s], 16 if o["dma"] else 1)
+    sent = ENG_PER_DST * RU * min(HB, len(T.cores) - 1 - rank)
+    if sent:
+        g.wait_ge(T.sem.loc, sent)
+    for s in sorted(total, key=lambda s: s == "st"):
+        g.wait_ge(T.sem[s], total[s])

@@ -1,19 +1,19 @@
+import numpy as np
 from concourse.bass import DstId, RemoteDMATransfer
 from concourse.mybir import AluOpType as ALU, ActivationFunctionType as ACT, AxisListType as AX
 
-P, W0, RU, HB, TW = 3072, 32, 3, 3, 4096
-CH = [512, 1024, 1024, 512]
-CD = [512, 1024, 1536]
-BIT = ["vvvv", "aavv", "aavv"]
-LOW = ["vvvv", "vvaa", "vvaa"]
-STEP = ["aaav", "aaav", "aaav"]
-BND = ["aaaa", "aaaa", "aaaa"]
-INV = ["avvv", "avvv", "aavv"]
-FLR = ["aaaa", "aaaa", "aaaa"]
-U, KF, KN = 2.0 ** -9, 24576.0, 49152.0
-ENG_PER_DST, GP = 4, 512
-CYC, PCY, LAT_X, LAT_S, GATH, XCH = 1.04, 0.52, 180.0, 90.0, 1.56, 3200.0
-ORDER = "IIiIhdhNhLhShMhMhMhLhLEGEDDBAAaAAZRKBTRAATMOQHAATRKChELXhBhKhHhOCaASELhKaGiahQBCdhDhDFcFZffaahIhAdJhHDiAHiOXZchChAaaeadGiAhdKhVFJWYIXhNFhVhThNRRARQEPPBOBNhHhBCBhDIDAbLLPJKOXLAILLQRKIIHIQDPGOANFMHTLSSHFHIIFMWXMHHHHIGJHINMHJKHFRFGZFVXFiRHMHFWKYXPUPTIJFMFGFFAHEGHHEEIIIFHhNHHFEhGLFSHHHHHEhDEFFhAEEEEEVYHMIFGEEHEBDLNAROLKJFDLHCALBKBJJEBHRHHNBGBBEBHUBGBBENONEWBDUBJBXBBGCNBECDQOOBNUBTDLODNBEBBJBBEBFFBHCBhRCAFAMCCABBEGEEBfcAbCCCAAEaaAAAADBQPYYSHWOSAAAEEABHHAAHBJJJAIAHQHCPOOEAAAABBHBBUFFQRAPbFOOYOPOEIADAFAOBHBGCJJJEIFCGEABDBAA"
+P, Q, W0, RU, HB, TW, NS, BANK = 3072, 1536, 32, 3, 3, 4096, 2, 512
+CUT = {"sign": "384 384 384 384", "scan": "768 768", "sel": "a480 a480 v576", "find": "1536", "low": "a256 a512 a512 a256",
+       "copy": "v384 a384 a384 a384", "bits": "768 768", "code": "768 768", "sum": "384 384 384 384", "floor": "a384 a384 a384 v384",
+       "out": "384 384 384 384"}
+LAST = {}
+KF, KN, NC, MAGIC, EVEN = 24576.0, 49152.0, -384.0, 1.5 * 2.0 ** 33, 1.5 * 2.0 ** 24
+ENG_PER_DST = 4
+PACES = [(0.95, 0.5, 1.45, 4000.0, 57.0, 75.0, 160.0, 85.0), (0.83, 0.415, 1.56, 3700.0, 50.0, 65.0, 150.0, 80.0),
+         (0.83, 0.45, 1.1, 4500.0, 50.0, 65.0, 200.0, 100.0), (1.2, 0.7, 1.7, 3500.0, 72.0, 95.0, 150.0, 80.0)]
+LEAD, OM, DL, BW, DGE = 3000.0, 3.0, 1300.0, 280.0, 1000.0
+ROUNDS, SEED = 1200, 1
+LOC = "vv"
 
 
 def _scratch():
@@ -22,104 +22,115 @@ def _scratch():
     def add(names, n, dt):
         for x in names.split():
             s[x] = ("sbuf", [128, n], dt)
-    for u in range(RU):
-        add("xw%d" % u, W0 + P, "bfloat16")
-        add("ws%d wka%d wkv%d" % (u, u, u), 144, "bfloat16")
-        add("mma%d mmv%d" % (u, u), 128, "bfloat16")
-        add("oh%d" % u, 512, "bfloat16")
-        add("summ%d" % u, 16, "int32")
-        add("land%d" % u, 48, "int32")
-    add("bt d0 lo fb nb yo ig", P, "bfloat16")
-    add("sel rr ss", P, "float16")
-    add("dd", P + 16, "float16")
-    add("bb", P, "float32")
-    add("tab", TW, "bfloat16")
-    add("fl", 1536, "bfloat16")
-    add("offk offi offc", 192, "uint16")
-    add("offs", 2, "uint16")
-    add("t1 t2 k16", 192, "bfloat16")
-    add("lc", 192, "float16")
+    for k in range(NS):
+        for u in range(RU):
+            n = "%d%d" % (k, u)
+            add("xw" + n, W0 + Q, "bfloat16")
+            add("lt" + n, 200, "bfloat16")
+            add("sm%s cb%s" % (n, n), 16, "float32")
+            add("land" + n, 64, "float32")
+        n = "%d" % k
+        add(" ".join(x + n for x in "lo fb nb yo got".split()), Q, "bfloat16")
+        add(" ".join(x + n for x in "sel rr ss bb".split()), Q, "float16")
+        add("dd" + n, Q + 16, "float16")
+        add("tile" + n, Q // 2, "float16")
+        add("tab" + n, TW, "bfloat16")
+        add("offi%s offc%s" % (n, n), 112, "uint16")
+        add("ia%s ib%s" % (n, n), 112, "int32")
+        add("mx" + n, 72, "float32")
+        add("lc" + n, 96, "float16")
+    add("ramp", Q, "float16")
+    add("ones", BANK, "float16")
     add("jr", 144, "float32")
-    add("gr gma gmv", 128, "float32")
-    add("pat", 640, "bfloat16")
-    add("id1 id16 ida idv id4k", 128, "bfloat16")
-    add("idh id2", 128, "float16")
-    add("en", 144, "float16")
-    add("pf pla plv em", 144, "bfloat16")
-    add("step", 48, "bfloat16")
-    add("pi", 4, "int32")
-    add("col q16 thr wkf hls", 16, "float32")
-    add("was kcs", 8, "bfloat16")
-    add("cmb", 48, "int32")
-    for b in range(8):
-        s["ps%d" % b] = ("psum", [128, 512], "float32")
+    add("vk pp id1 ida idv", 128, "bfloat16")
+    add("vs as", 72, "bfloat16")
+    add("gcol msk", 256, "bfloat16")
+    add("fm sm", 256, "float16")
+    add("pf em", 144, "bfloat16")
+    add("kz", 112, "bfloat16")
+    add("pi", 8, "int32")
+    add("col q16 cw ck hls bz", 16, "float32")
+    add("wk", 8, "bfloat16")
+    s["ps"] = ("psum", [128, 8 * BANK], "float32")
     return s
 
 
 SCRATCH = _scratch()
-SEMAPHORES = ["ev", "ea", "ep", "eg", "loc", "st", "arr0", "arr1", "arr2"] + ["dm%d" % i for i in range(12)]
+SEMAPHORES = ["ev", "ea", "ep", "eg", "loc", "st"] + ["arr%d" % i for i in range(NS * RU)] + ["dm%d" % i for i in range(24)] + ["ad%d" % i for i in range(24)]
 ENGSEM = {"v": "ev", "a": "ea", "p": "ep", "g": "eg"}
 
 
-def _cuts(sizes):
-    return [(sum(sizes[:i]), sum(sizes[:i + 1])) for i in range(len(sizes))]
+def _cuts(text):
+    out, a = [], 0
+    for x in text.split():
+        n = int(x.lstrip("av"))
+        out.append((x[0], a, a + n))
+        a += n
+    return out
 
 
-def _pieces(a, b, m=512):
-    n = (b - a + m - 1) // m
-    return [(a + i * (b - a) // n, a + (i + 1) * (b - a) // n) for i in range(n)]
+def _banked(a, b):
+    return [(c - a, c, min(c + BANK, b)) for c in range(a, b, BANK)]
 
 
-def _program(g, T, topo, rank):
-    ops, hist, at, nd = [], {}, ["c0", 0, 0], [0]
+def R(b, lo, hi, p0=0, p1=128, st=1):
+    return ("r", b, lo, hi, p0, p1, st)
+
+
+def PS(tok, lo, hi, p0=0, p1=128, st=1):
+    return ("p", tok, lo, hi, p0, p1, st)
+
+
+def IX(win, off):
+    return ("i", win, off)
+
+
+def _program(g, T, topo, rank, pace):
+    CYC, PCY, GATH, XCH, OV, OA = pace[:6]
+    ops, hist, nd, now = [], {}, [0], [0]
     V, A, PE = g.vector, g.scalar, g.tensor
-
-    def stage(name, u=0, n=0):
-        at[0], at[1], at[2] = name, n, u
 
     def op(eng, cost, fn, rd=(), wr=(), tok=None, soft=(), dma=None, lat=0.0, pre=None):
         i = len(ops)
         deps = set()
         for (lst, is_w) in ((rd, False), (wr, True)):
-            for (b, lo, hi) in lst:
-                deps |= {j for (j, l2, h2, w2) in hist.get(b, ()) if (is_w or w2) and l2 < hi and lo < h2}
+            for r in lst:
+                deps |= {j for (j, q, w2) in hist.get(r[1], ()) if (is_w or w2) and q[2] < r[3] and r[2] < q[3] and q[4] < r[5] and r[4] < q[5]}
         for (lst, is_w) in ((rd, False), (wr, True)):
-            for (b, lo, hi) in lst:
-                h = hist.setdefault(b, [])
+            for r in lst:
+                h = hist.setdefault(r[1], [])
                 if is_w:
-                    h[:] = [e for e in h if not (lo <= e[1] and e[2] <= hi)]
-                h.append((i, lo, hi, is_w))
+                    h[:] = [e for e in h if not (r[2] <= e[1][2] and e[1][3] <= r[3] and r[4] <= e[1][4] and e[1][5] <= r[5])]
+                h.append((i, r, is_w))
         if tok is not None:
             deps |= {j for j in tok["ops"] if ops[j]["e"] != eng}
             soft = list(soft) + tok["ops"][-1:]
             tok["ops"].append(i)
         deps.discard(i)
         ops.append({"e": eng, "c": cost, "fn": fn, "deps": deps, "soft": set(soft) - deps, "tok": tok, "dma": dma, "lat": lat,
-                    "pre": pre, "key": "%s.%d" % (at[0], at[1]), "u": at[2]})
-        at[1] += 1
+                    "pre": pre, "s": now[0]})
         return i
 
-    def token(kind):
-        return {"kind": kind, "ops": [], "b": None}
+    def token(w):
+        return {"ops": [], "b": None, "n": (w + BANK - 1) // BANK}
 
     def ap(x):
         if not isinstance(x, tuple):
             return x
-        if len(x) == 2:
-            return T["ps%d" % x[0]["b"]][:, 0:x[1]]
-        if len(x) == 6:
-            return T[x[0]][:, x[1]:x[2]].indirect(T[x[3]][:, x[4]:x[5]])
-        return T[x[0]][:, x[1]:x[2]]
+        if x[0] == "i":
+            return ap(x[1]).indirect(ap(x[2]))
+        t, c = (T.ps, BANK * x[1]["b"]) if x[0] == "p" else (T[x[1]], 0)
+        return t[x[4]:x[5], c + x[2]:c + x[3]:x[6]] if x[6] > 1 else t[x[4]:x[5], c + x[2]:c + x[3]]
 
     def call(eng, f, fn, out, args, tail=(), kw=None, **k):
         rd, tok = [], None
         for x in list(args) + list((kw or {}).values()):
             if isinstance(x, tuple):
-                if len(x) == 2:
-                    tok = x[0]
+                if x[0] == "p":
+                    tok = x[1]
                 else:
-                    rd += [x[0:3]] + ([x[3:6]] if len(x) == 6 else [])
-        cost = max(64.0, (out[2] - out[1]) * f) * CYC + (30.0 if eng == "v" else 60.0)
+                    rd += [x] if x[0] == "r" else [x[1], x[2]]
+        cost = max(64.0, (out[3] - out[2]) * f) * CYC + (OV if eng == "v" else OA)
         return op(eng, cost, lambda: fn(ap(out), *[ap(x) for x in args], *tail, **{q: ap(x) for q, x in (kw or {}).items()}),
                   rd, [out], tok=tok, **k)
 
@@ -129,275 +140,416 @@ def _program(g, T, topo, rank):
     def tt(out, in0, in1, o, f=1.0, **k):
         return call("v", f, V.tensor_tensor, out, [in0, in1], [o], **k)
 
-    def act(out, in_, func, f=1.0, **kw):
-        return call("a", f, A.activation, out, [in_], [func], kw)
+    def act(out, in_, func, f=1.0, soft=(), **kw):
+        return call("a", f, A.activation, out, [in_], [func], kw, soft=soft)
 
     def mset(out, val):
         return call("v", 0.5, V.memset, out, [val])
 
-    def mm(tok, n, items, start=True, stop=True, **k):
-        rd, cnt = [], 0
-        for it in items:
-            rd += [it[0], it[1]] if len(it) == 2 else [(it[0], 0, 144), it[1:]]
-            cnt += 1 if len(it) == 2 else 16
+    def lin(out, in_, scale, bias):
+        return act(out, in_, ACT.Identity, scale=scale, bias=bias)
+
+    def fill(out, val):
+        return lin(out, R("vk", 0, out[3] - out[2], out[4], out[5]), 0.0, val)
+
+    def copy(eng, out, in_):
+        return act(out, in_, ACT.Identity) if eng == "a" else call("v", 1.0, V.tensor_copy, out, [in_])
+
+    def skip(eng, soft=()):
+        return op(eng, 0.0, None, soft=soft)
+
+    def mm(groups, **k):
+        items = [it for grp in groups for it in grp]
+        cost = sum(max(64, (it[0][3] - it[0][2] + it[0][6] - 1) // it[0][6]) for it in items) * PCY + 20.0 + OM * len(items)
 
         def fn():
-            prs = []
-            for it in items:
-                prs += [(ap(it[0]), ap(it[1]))] if len(it) == 2 else [
-                    (T[it[0]][:, 15 - i:143 - i], T[it[1]][:, it[2] + i:it[3]:16]) for i in range(16)]
-            for q, (lhs, rhs) in enumerate(prs):
-                last = PE.matmul(ap((tok, n)), lhs, rhs, start and q == 0, stop and q == len(prs) - 1)
+            for grp in groups:
+                for q, (o, lhs, rhs) in enumerate(grp):
+                    last = PE.matmul(ap(o), ap(lhs), ap(rhs), q == 0, q == len(grp) - 1)
             return last
-        return op("p", cnt * max(64, n) * PCY + 20.0, fn, rd, (), tok=tok, **k)
+        return op("p", cost, fn, [x for it in items for x in it[1:]], (), tok=items[0][0][1], **k)
 
-    def iota(out, pattern, base, cm, **kw):
-        return op("g", 160.0 + 2 * CYC * (out[2] - out[1]), lambda: g.iota(ap(out), pattern, base, cm, **kw), (), [out])
+    def compact(tok, c0, w, src, a, b):
+        return [(PS(tok, c0, c0 + (b - a) // 16), R(w, 15 - i, 143 - i), R(src, a + i, b, st=16)) for i in range(16)]
+
+    def summed(a, b, parts, **k):
+        tk = token(b - a)
+        mm([[(PS(tk, c, c + y - x), whole(m), R(src, c0 + x, c0 + y)) for (m, src, c0) in parts] for (c, x, y) in _banked(a, b)], **k)
+        return PS(tk, 0, b - a)
+
+    def iota(out, pattern, base, cm=0):
+        kw = {} if out[1] == "pi" else {"allow_small_or_imprecise_dtypes": True}
+        return op("g", 160.0 + 2 * CYC * (out[3] - out[2]), lambda: g.iota(ap(out), pattern, base, cm, **kw), (), [out])
 
     def dma(eng, out, in_, rd, wr, nbytes, sem=None):
         if sem is None:
             sem = "dm%d" % nd[0]
             nd[0] += 1
         q = g.sync if eng == "s" else g.scalar
-        return op(eng, 60.0, lambda: q.dma_start(out, in_), rd, wr, dma=sem, lat=1900.0 + nbytes / 300.0)
+        return op(eng, 60.0, lambda: q.dma_start(out, in_), rd, wr, dma=sem, lat=DL + nbytes / BW)
 
-    def col(i, b="col"):
-        return (b, i, i + 1)
+    def col(i, p0=0, p1=128, b="col"):
+        return R(b, i, i + 1, p0, p1)
 
-    def whole(b):
-        return (b, 0, 128)
+    def whole(b, n=128):
+        return R(b, 0, n)
 
-    ch, small = _cuts(CH), {"allow_small_or_imprecise_dtypes": True}
-    add, mul, eq = ALU.add, ALU.mult, ALU.is_equal
-    dma("a", T.kcs[:, 0:3], T.kc[:, :], (), [("kcs", 0, 8)], 0)
-    dma("a", T.was[:, 0:3], T.wa[:, :], (), [("was", 0, 8)], 0)
-    dma("a", T.hls[:, 0:6], T.hl[:, :], (), [("hls", 0, 8)], 0)
-    for (a, b) in ch:
-        dma("s", T.xw0[:, W0 + a:W0 + b], T.x[:, a:b], (), [("xw0", W0 + a, W0 + b)], b * 256)
-    dma("s", T.tab[:, :], T.inv[:, :], (), [("tab", 0, TW)], (P + TW) * 256)
+    add, mul, eq, sub = ALU.add, ALU.mult, ALU.is_equal, ALU.subtract
+    halves = [(h, 64 * h, 64 * h + 64) for h in range(2)]
+    first = [_cuts("512 1024"), _cuts("1536")]
 
-    jr, kc3 = ("jr", 0, 144), ("kcs", 0, 3)
-    iota(("pi", 0, 1), [[0, 1]], 0, 1)
-    iota(jr, [[1, 144]], 0, 0, **small)
-    ts(("pi", 1, 2), ("pi", 0, 1), 15, ALU.bitwise_and)
-    call("v", 1.0, V.tensor_copy, ("col", 0, 2), [("pi", 0, 2)])
-    ts(col(3), col(0), col(1), ALU.subtract)
-    ts(col(2), col(0), col(1), ALU.subtract, 15.0, add)
-    ts(("em", 0, 144), jr, col(2), eq)
-    act(("wkf", 0, 3), ("was", 0, 3), ACT.Identity)
-    act(("wkf", 4, 7), kc3, ACT.Identity)
-    act(("wkf", 8, 11), kc3, ACT.Identity, scale=2.0)
-    ts(("thr", 0, 3), kc3, 0.0, eq, 0.75, ALU.subtract)
-    ts(("thr", 12, 15), kc3, 1.0, ALU.min, 128.0, mul)
-    act(("thr", 4, 7), ("hls", 3, 6), ACT.Identity, scale=-1.0, bias=-0.5)
-    act(("thr", 8, 11), ("hls", 0, 3), ACT.Identity, scale=-1.0, bias=0.5)
+    dma("a", T.wk[:, 3:6], T.kc[:, :], (), [R("wk", 3, 6)], 0)
+    dma("a", T.wk[:, 0:3], T.wa[:, :], (), [R("wk", 0, 3)], 0)
+    for k in range(NS):
+        for y in range(2):
+            dma("a", T.hls[64 + 16 * y:80 + 16 * y, 3 * k:3 * k + 3], T.hl[64 * k:64 * k + 64:4, 3 * y:3 * y + 3], (),
+                [R("hls", 3 * k, 3 * k + 3, 64 + 16 * y, 80 + 16 * y)], 0)
+    done = 0
+    for k in range(NS):
+        for (_, a, b) in first[k]:
+            for (h, p0, p1) in halves:
+                done += (b - a) * 128
+                dma("s", T["xw%d0" % k][p0:p1, W0 + a:W0 + b], T.x[64 * k:64 * k + 64, Q * h + a:Q * h + b], (),
+                    [R("xw%d0" % k, W0 + a, W0 + b, p0, p1)], done)
+    for k in range(NS):
+        for (h, p0, p1) in halves:
+            done += TW * 128
+            dma("s", T["tab%d" % k][p0:p1, :], T.inv[64 * k:64 * k + 64, :], (), [R("tab%d" % k, 0, TW, p0, p1)], done)
+
+    jr = R("jr", 0, 144)
+    iota(R("pi", 0, 1), [[0, 1]], 0, 1)
+    for j in range(4):
+        iota(R("vk", 32 * j, 32 * j + 32), [[1, 16], [-1, 2]], 16 << j)
+    iota(R("vs", 0, 64), [[0, 2], [1, 16], [-1, 2]], 0)
+    iota(R("vs", 64, 66), [[0, 2]], -5)
+    for e in range(2):
+        iota(R("gcol", 128 * e, 128 * e + 128), [[2, 2], [4, 4], [0, 16]], e)
+    for j in (3, 2, 1, 0):
+        iota(R("pp", 0, 128, 0, 16 * j + 16), [[0, 64 >> j], [4096, 2], [0, 1 << j]], -2048)
+    iota(jr, [[1, 144]], 0)
+    ts(R("pi", 1, 2), R("pi", 0, 1), 15, ALU.bitwise_and)
+    ts(R("pi", 2, 3), R("pi", 0, 1), 2, ALU.logical_shift_right, 12, ALU.bitwise_and)
+    ts(R("pi", 3, 4), R("pi", 0, 1), 5, ALU.logical_shift_right, 2, ALU.bitwise_and)
+    copy("v", R("col", 0, 4), R("pi", 0, 4))
+    lin(col(5), col(2), 1.0, col(3))
+    for k in range(NS):
+        for (h, p0, p1) in halves:
+            copy("a", R("cw", 8 * k, 8 * k + 6, p0, p1), R("wk", 0, 6, 64 * k, 64 * k + 64))
+        lin(R("ck", 4 * k, 4 * k + 3), R("cw", 8 * k + 3, 8 * k + 6), 16.0, col(5))
+    ts(R("as", 0, 66), R("vs", 0, 66), col(5), eq)
+    ts(col(7, 64, 96), col(0, 64, 96), 80.0, ALU.is_lt, 0.5, sub)
+    lin(col(8, 64, 96), col(7, 64, 96), 14336.0, -5120.0)
+    lin(col(9, 64, 96), col(7, 64, 96), -2048.0, 1024.0)
+    fill(R("bz", 0, 8, 0, 64), -127.5)
+    fill(R("bz", 0, 8, 96, 97), 1.0)
+    lin(R("bz", 0, 6, 64, 96), R("hls", 0, 6, 64, 96), -1.0, col(7, 64, 96))
+    ts(R("msk", 0, 256, 0, 64), R("gcol", 0, 256, 0, 64), col(1, 0, 64), eq, f=0.5)
+    for e in range(2):
+        tt(R("fm", 128 * e, 128 * e + 128, 0, 64), R("msk", 128 * e, 128 * e + 128, 0, 64), R("pp", 0, 128, 0, 64), mul)
+    copy("a", R("sm", 0, 256, 0, 64), R("fm", 0, 256, 0, 64))
+    ts(R("fm", 0, 256, 64, 96), R("gcol", 0, 256, 64, 96), col(1, 64, 96), eq, col(8, 64, 96), mul, 0.5)
+    ts(R("sm", 0, 256, 64, 96), R("gcol", 0, 256, 64, 96), col(1, 64, 96), eq, col(9, 64, 96), mul, 0.5)
+    mset(R("fm", 0, 256, 96, 98), 1.0)
+    fill(R("fm", 0, 128, 96, 97), 2046.0)
+    fill(R("fm", 128, 256, 96, 97), 2048.0)
+    mset(R("sm", 0, 256, 96, 97), -8192.0)
+    mset(R("ones", 0, BANK), 1.0)
+    for (_, a, b) in _banked(0, Q):
+        call("v", 0.5, V.tensor_tensor_scan, R("ramp", a, b), [R("ones", 0, BANK), R("ones", 0, BANK), 2.0 * a - 1521.0], [add, add])
+    for k in range(NS):
+        now[0] = k
+        for (_, a, b) in first[k]:
+            ts(R("tile%d" % k, a // 2, b // 2, 96, 98), R("ramp", a, b, 96, 98, 2), 1.0, add, f=0.5)
+        lin(R("dd%d" % k, 0, 1), col(1), 2.0, 32.0 - 1584.0)
+    now[0] = 0
+    ts(col(4), col(0), col(1), sub, 15.0, add)
+    lin(col(6), col(3), 512.0, 1024.0 * (2 * rank + 1))
+    ts(R("em", 0, 144), jr, col(4), eq)
     ts(whole("id1"), whole("jr"), col(0), eq)
-    for (b, v) in (("id16", 16.0), ("ida", 256.0), ("idv", 512.0), ("id4k", 4096.0)):
-        act(whole(b), whole("id1"), ACT.Identity, scale=v)
-    ts(whole("idh"), whole("id1"), 1.0, mul, f=0.5)
-    ts(whole("id2"), whole("id1"), 2.0, mul, f=0.5)
-    ts(col(4), col(1), 16.0, add)
-    ts(col(5), col(1), -U, mul, (15 - 2048) * U, add)
-    ts(col(6), col(1), float(W0 - 1 - 2048 - 49 * 2048 - 4096), add)
-    ts(("dd", 0, 1), col(1), -U, mul, (15 - 2048) * U, add)
-    mset(("step", 0, 16), 8.0)
-    ts(("step", 16, 48), ("jr", 0, 32), col(4), eq, -65536.0, mul)
-    ts(("step", 16, 48), ("step", 16, 48), U, add)
-    mset(("fl", 0, max(CH)), -4.0)
-    ts(("en", 0, 144), ("em", 0, 144), -512.0, mul, f=0.5)
-    ts(("q16", 0, 16), ("jr", 0, 16), col(1), ALU.is_lt, 1.0, add)
-    call("v", 1.0, V.tensor_reduce, col(7), [("q16", 0, 16)], [AX.X, mul])
-    ts(col(8), col(1), 12.0, ALU.is_lt)
-    ts(col(9), col(7), col(8), mul, 1.0 / 128, mul)
-    act(("pf", 0, 144), ("em", 0, 144), ACT.Identity, scale=col(9))
-    act(("pla", 0, 144), ("pf", 0, 144), ACT.Identity, scale=-64.0)
-    act(("plv", 0, 144), ("pf", 0, 144), ACT.Identity, scale=-128.0)
-    iota(whole("gr"), [[16, 8], [0, 16]], 0, 0, **small)
-    for b in range(4):
-        iota(("pat", 128 * b, 128 * b + 128), [[0, 64 >> b], [8, 2], [0, 1 << b]], -3, 0, **small)
-    iota(("pat", 512, 640), [[0, 128]], -1, 0, **small)
-    iota(("k16", 0, 192), [[16, 192]], 0, 0, **small)
-    ts(whole("gma"), whole("gr"), col(3), eq)
-    act(whole("gmv"), whole("gma"), ACT.Identity, scale=2.0)
-    for u in range(RU):
-        stage("M%d" % u)
-        iota(("xw%d" % u, 0, 32), [[-15872, 2], [0, 16]], -512, 0, **small)
-        act(("ws%d" % u, 0, 144), ("em", 0, 144), ACT.Identity, scale=col(u, "wkf"))
-        tk = token("m")
-        oh = [("oh%d" % u, 128 * b, 128 * b + 128) for b in range(4)]
-        for b in range(4):
-            ts(oh[b], whole("id1"), col(4 + u, "wkf"), mul, float(1 << b), eq, 0.5)
-        mm(tk, 128, [(oh[b], ("pat", 128 * b, 128 * b + 128)) for b in range(4)] + [(whole("id1"), ("pat", 512, 640))])
-        for e in sorted(set(BIT[u])):
-            act(("wk%s%d" % (e, u), 0, 144), ("em", 0, 144), ACT.Identity, scale=col((4 if e == "a" else 8) + u, "wkf"))
-            tt(whole("mm%s%d" % (e, u)), (tk, 128), whole("gm" + e), mul)
+    ts(R("q16", 0, 16), R("jr", 0, 16), col(1), ALU.is_lt, 1.0, add)
+    call("v", 1.0, V.tensor_reduce, col(11), [R("q16", 0, 16)], [AX.X, mul])
+    ts(col(12), col(1), 12.0, ALU.is_lt, 1.0 / 256, mul)
+    ts(R("pf", 0, 144), R("em", 0, 144), col(11), mul, col(12), mul, 0.5)
+    for (e, v) in (("a", 256.0), ("v", 512.0)):
+        if e in CUT["low"] + LAST.get("low", ""):
+            lin(whole("id" + e), whole("id1"), v, 0.0)
+    for (e, v) in (("a", -1600), ("v", 100352)):
+        mine = [c for c in _cuts(CUT["sel"]) if c[0] == e]
+        if mine:
+            iota(R("kz", mine[0][1] // 16, mine[-1][2] // 16), [[0, (mine[-1][2] - mine[0][1]) // 16]], v)
 
-    def rule(u):
-        xw = "xw%d" % u
-        for j, (a, b) in enumerate(ch):
-            stage("A%d" % j, u)
-            ka, kb, n = a // 16, b // 16, (b - a) // 16
-            t_s, t_k = token("s"), token("k")
-            mm(t_s, n, [("ws%d" % u, xw, W0 + a, W0 + b)])
-            act(("t1", ka, kb), (t_s, n), ACT.Sign, bias=col(4 + u, "thr"))
-            act(("t2", ka, kb), (t_s, n), ACT.Sign, bias=col(8 + u, "thr"))
-            if BIT[u][j] == "v":
-                ts(("bt", a, b), (xw, W0 + a, W0 + b), col(12 + u, "thr"), ALU.is_ge, 0.5, ALU.subtract, 0.5)
+    def setup(k, u):
+        n = "%d%d" % (k, u)
+        ts(R("lt" + n, 0, 128), whole("vk"), col(4 * k + u, b="ck"), eq, f=0.5)
+        lin(R("lt" + n, 128, 194), R("as", 0, 66), col(8 * k + u, b="cw"), 0.0)
+        iota(R("xw" + n, 0, 32), [[-32384, 2], [0, 16]], int(NC))
+        iota(R("land" + n, 48, 64, 0, 64), [[0, 16]], int(NC))
+
+    def rule(k, u):
+        n, z = "%d%d" % (k, u), NS * u + k
+        cut = {x: _cuts(LAST.get(x, y) if u == RU - 1 else y) for x, y in CUT.items()}
+        xw, tile, dd = "xw" + n, "tile%d" % k, "dd%d" % k
+        lo, fb, nb, yo, got, sel, rr, ss, bb, tab, offi, offc, ia, ib, mx, lc = [
+            "%s%d" % (x, k) for x in "lo fb nb yo got sel rr ss bb tab offi offc ia ib mx lc".split()]
+        window = R(xw, 0, W0 + Q)
+
+        def form(tk, w, rows, c, x, y):
+            return [(PS(tk, c + e, c + y - x, st=2), R(w, 128 * e, 128 * e + 128, 0, rows), R(tile, x // 2, y // 2, 0, rows)) for e in range(2)]
+        for (_, a, b) in cut["sign"]:
+            w = (b - a) // 2
+            tk = token(w)
+            mm([[(PS(tk, c, c + y - x, 0, 97), R("lt" + n, e, 194, st=2), R(xw, W0 + 2 * x + e, W0 + 2 * y, st=2)) for e in range(2)]
+                for (c, x, y) in _banked(a // 2, b // 2)])
+            act(R(tile, a // 2, b // 2, 0, 97), PS(tk, 0, w, 0, 97), ACT.Sign, bias=col(3 * k + u, 0, 97, "bz"))
+        for (_, a, b) in cut["scan"]:
+            tk = token(b - a)
+            mm([[m] for run in _banked(a, b) for m in form(tk, "fm", 98, *run)])
+            call("v", 1.0, V.tensor_tensor_scan, R(dd, a + 1, b + 1), [PS(tk, 0, b - a), R("ramp", a, b), R(dd, a, a + 1)], [ALU.max, ALU.min])
+        end, even, half = R(dd, Q, Q + 1), R(mx, 64, 65), R(mx, 68, 69)
+        ts(even, end, EVEN, add, EVEN, sub)
+        lin(half, end, 0.5, 792.0)
+        ts(R(offi, 96, 97), end, even, eq, half, mul)
+        for (e, a, b) in cut["sel"]:
+            tk = token(b - a)
+            if e == "a":
+                mm([[(PS(tk, c, c + y - x), whole("id1"), R(dd, x, y))] + form(tk, "sm", 97, c, x, y) for (c, x, y) in _banked(a, b)])
+                act(R(sel, a, b), PS(tk, 0, b - a), ACT.Relu, bias=-448.0)
             else:
-                for (pa, pb) in _pieces(a, b):
-                    act(("bt", pa, pb), (xw, W0 + pa, W0 + pb), ACT.Sign, bias=col(u, "thr"), scale=1.0 / 170)
-            stage("A%d" % j, u, 10)
-            mm(t_k, n, [("wk%s%d" % (BIT[u][j], u), "bt", a, b)], True, False)
-            mm(t_k, n, [(whole("id16"), ("t1", ka, kb)), (whole("id16"), ("t2", ka, kb))], False, True)
-            ts(("offk", ka, kb), (t_k, n), 0.5, mul, 23.5, add)
-            src = ("step", 0, 48, "offk", ka, kb)
-            if STEP[u][j] == "a":
-                act(("d0", a, b), src, ACT.Identity, GATH)
-            else:
-                call("v", GATH, V.tensor_copy, ("d0", a, b), [src])
-            sent = call("v", 0.5, V.tensor_tensor_scan, ("dd", a + 1, b + 1), [("d0", a, b), ("fl", 0, b - a), ("dd", a, a + 1) if a else col(5)],
-                        [add, ALU.max])
-        stage("S0", u)
+                mm([[m] for run in _banked(a, b) for m in form(tk, "sm", 97, *run)], soft=[h[0] for h in hist[dd] if h[2] and h[1][2] <= a < h[1][3]])
+                tt(R(sel, a, b), R(dd, a, b), PS(tk, 0, b - a), ALU.min)
+        for (_, a, b) in cut["find"]:
+            ka, kb = a // 16, b // 16
+            tk = token(kb - ka)
+            mm([[(PS(tk, 0, kb - ka), whole("id1"), R("kz", ka, kb))] + compact(tk, 0, "em", sel, a, b)])
+            ts(R(ia, ka, kb), PS(tk, 0, kb - ka), 2047.5, mul, 808.25, add)
+            ts(R(ib, ka, kb), R(ia, ka, kb), 4095, ALU.bitwise_and)
+            found = ts(R(offi, ka, kb), R(ib, ka, kb), -1.0, mul, 1600.0, add)
+        sm, cb, land = "sm" + n, "cb" + n, "land" + n
+        sent = ts(R(sm, 0, 16), IX(window, R(offi, 96, 97)), col(6), add, NC, ALU.max)
+        copy(LOC[0], R(land, 48, 64, 64, 128), R(sm, 0, 16, 0, 64))
         dsts = [rank + d for d in range(1, HB + 1) if rank + d < len(T.cores)]
         if dsts:
-            sm = ("summ%d" % u, 0, 16)
-            ts(("offs", 0, 1), ("dd", P, P + 1), -512.0, mul, float(P - 1 + W0 - 2048), add)
-            ts(sm, (xw, 0, W0 + P, "offs", 0, 1), float(512 + 1024 * (rank + 1)), add, 0.0, ALU.max)
+            tt(R(cb, 0, 16, 64, 128), R(sm, 0, 16, 64, 128), R(land, 48, 64, 64, 128), ALU.max)
+            copy(LOC[1], R(cb, 0, 16, 0, 64), R(cb, 0, 16, 64, 128))
+        else:
+            skip("v")
+            skip(LOC[1])
 
-            def send():
-                trs = []
-                for q, r2 in enumerate(dsts):
-                    rid, pid = topo.addr(T.cores[r2])[:2]
-                    eng = topo.engines(T.cores[rank], T.cores[r2])[q * ENG_PER_DST:(q + 1) * ENG_PER_DST]
-                    trs.append(RemoteDMATransfer(dst_ids=[DstId(rid=rid, pnc=pid)], dma_engine_mask=sum(1 << e for e in eng),
-                                                 remote_sem=T.sem["arr%d" % u], src=ap(sm), dst=ap(("land%d" % u, 16 * q, 16 * q + 16))))
-                g.remote_dma_fused(trs, local_sem=T.sem.loc)
-            sent = op("g", 1000.0, send, [sm], (), lat=XCH - 1000.0)
-        for j, (a, b) in enumerate(ch):
-            stage("D%d" % j, u)
-            for (pa, pb) in _pieces(a, b):
-                tk = token("mm")
-                mm(tk, pb - pa, [(whole("mm%s%d" % (BIT[u][j], u)), ("bt", pa, pb))], soft=[e[0] for e in hist["d0"] if e[1] < pb and pa < e[2]])
-                tt(("sel", pa, pb), ("dd", pa, pb), (tk, pb - pa), ALU.min)
-        for j, (a, b) in enumerate(_cuts(CD)):
-            stage("I%d" % j, u)
-            ka, kb, tk = a // 16, b // 16, token("i")
-            mm(tk, kb - ka, [(whole("id1"), ("k16", ka, kb)), (whole("id4k"), ("t1", ka, kb)), ("en", "sel", a, b)])
-            ts(("offi", ka, kb), (tk, kb - ka), col(6), add, 0.0, ALU.max)
-        for j, (a, b) in enumerate(ch):
-            stage("L%d" % j, u)
-            ka, kb, e = a // 16, b // 16, LOW[u][j]
-            for (pa, pb) in _pieces(a, b):
-                xs, tk = (xw, W0 + pa, W0 + pb), token("b")
-                if e == "a":
-                    act(("lo", pa, pb), xs, ACT.Sign, bias=-63.5)
-                else:
-                    ts(("lo", pa, pb), xs, 64.0, ALU.is_ge, 0.5, ALU.subtract, 0.5)
-                mm(tk, pb - pa, [(whole("id1"), xs), (whole("id" + e), ("lo", pa, pb))])
-                if BND[u][j] == "a":
-                    act(("bb", pa, pb), (tk, pb - pa), ACT.Identity)
-                else:
-                    call("v", 1.0, V.tensor_copy, ("bb", pa, pb), [(tk, pb - pa)])
-            if j % 2:
-                a = ch[j - 1][0]
-                tk = token("b")
-                mm(tk, (b - a) // 16, [("pl" + e, "lo", a, b)])
-                ts(("lc", a // 16, kb), (tk, (b - a) // 16), 0.5, add)
-        stage("R0", u)
+        def send():
+            trs = []
+            for q, r2 in enumerate(dsts):
+                rid, pid = topo.addr(T.cores[r2])[:2]
+                eng = topo.engines(T.cores[rank], T.cores[r2])[q * ENG_PER_DST:(q + 1) * ENG_PER_DST]
+                trs.append(RemoteDMATransfer(dst_ids=[DstId(rid=rid, pnc=pid)], dma_engine_mask=sum(1 << e for e in eng),
+                                             remote_sem=T.sem["arr%d" % z], src=ap(R(cb, 0, 16)), dst=ap(R(land, 16 * q, 16 * q + 16))))
+            g.remote_dma_fused(trs, local_sem=T.sem.loc)
+        sent = op("g", 1000.0, send if dsts else None, [R(cb, 0, 16)] if dsts else (), (), soft=[sent], lat=XCH - 1000.0)
+
+        def bound(a, b, **k2):
+            e = [c[0] for c in cut["low"] if c[1] <= a < c[2]][0]
+            return summed(a, b, [("id1", xw, W0), ("id" + e, lo, 0)], **k2)
+        runs = []
+        for (e, a, b) in cut["low"]:
+            if e == "a":
+                act(R(lo, a, b), R(xw, W0 + a, W0 + b), ACT.Sign, bias=-63.5)
+            else:
+                ts(R(lo, a, b), R(xw, W0 + a, W0 + b), 64.0, ALU.is_ge, 0.5, sub, 0.5)
+            if runs and runs[-1][0] == e:
+                runs[-1][2] = b
+            else:
+                runs.append([e, a, b])
+        for (e, a, b) in cut["copy"]:
+            if e == "v":
+                copy("a", R(bb, a, b), bound(a, b))
+        for (e, a, b) in runs:
+            tk = token((b - a) // 16)
+            mm([compact(tk, 0, "pf", lo, a, b)])
+            lin(R(lc, a // 16, b // 16), PS(tk, 0, (b - a) // 16), -128.0 if e == "a" else -256.0, 0.5)
         ns = min(rank, HB)
-        if ns:
-            pre, src = ("arr%d" % u, ENG_PER_DST * ns), ("land%d" % u, 0, 16)
-            for q in range(1, ns):
-                dst = ("cmb", 16 * q - 16, 16 * q)
-                tt(dst, src, ("land%d" % u, 16 * q, 16 * q + 16), ALU.max, soft=[sent], pre=pre)
-                src, pre = dst, None
-            ts(("cmb", 32, 48), src, 1023, ALU.bitwise_and, soft=[sent], pre=pre)
-            ts((xw, 16, 32), ("cmb", 32, 48), -512.0, add)
-        nx, no = ("yo", 0) if u == RU - 1 else ("xw%d" % (u + 1), W0)
-        for j, (a, b) in enumerate(ch):
-            stage("B%d" % j, u)
-            ka, kb, tk = a // 16, b // 16, token("c")
-            for (pa, pb) in _pieces(a, b, GP):
-                tt(("rr", pa, pb), (xw, 0, W0 + P, "offi", pa // 16, pb // 16), ("bb", pa, pb), ALU.max, GATH, soft=[sent])
-                ts(("fb", pa, pb), ("rr", pa, pb), 0.0, ALU.max, KF - 63.5, add, 0.5)
-            mm(tk, kb - ka, [(whole("id2"), ("lc", ka, kb)), ("pf", "fb", a, b)])
-            ts(("offc", ka, kb), (tk, kb - ka), -(KF / 128 + 1) * 4095 - 1, add)
-            stage("B%d" % j, u, 10)
-            for (pa, pb) in _pieces(a, b, GP):
-                src = ("tab", 0, TW, "offc", pa // 16, pb // 16)
-                if INV[u][j] == "v":
-                    tt(("ss", pa, pb), src, ("rr", pa, pb), add, GATH)
-                    ts(("nb", pa, pb), ("ss", pa, pb), -1.0, mul, 127.5 - KN, add, 0.5)
-                else:
-                    act(("ig", pa, pb), src, ACT.Identity, GATH)
-            stage("B%d" % j, u, 20)
-            for (pa, pb) in _pieces(a, b):
-                tk, w = token("x"), pb - pa
-                if INV[u][j] == "v":
-                    mm(tk, w, [(whole("idh"), ("ss", pa, pb)), (whole("id1"), ("nb", pa, pb))])
-                else:
-                    both = [(whole("idh"), ("rr", pa, pb)), (whole("id1"), ("ig", pa, pb))]
-                    mm(tk, w, both)
-                    if FLR[u][j] == "a":
-                        act(("nb", pa, pb), (tk, w), ACT.Identity, scale=-1.0, bias=127.5 - KN)
-                    else:
-                        ts(("nb", pa, pb), (tk, w), -1.0, mul, 127.5 - KN, add)
-                    tk = token("x")
-                    mm(tk, w, both + [(whole("id1"), ("nb", pa, pb))])
-                act((nx, no + pa, no + pb), (tk, w), ACT.Identity, bias=KN)
-                if u == RU - 1:
-                    dma("s", T.y[:, pa:pb], T.yo[:, pa:pb], [("yo", pa, pb)], (), w * 256, sem="st")
+        pre, src = (("arr%d" % z, ENG_PER_DST * ns) if ns else None), R(land, 48, 64)
+        if ns == 3:
+            tt(R(mx, 0, 32), R(land, 0, 32), R(land, 32, 64), ALU.max, soft=[sent], pre=pre)
+            tt(R(mx, 32, 48), R(mx, 0, 16), R(mx, 16, 32), ALU.max)
+            src = R(mx, 32, 48)
+        else:
+            for q in range(ns):
+                tt(R(mx, 16 * q, 16 * q + 16), R(land, 16 * q, 16 * q + 16), src, ALU.max, soft=[sent], pre=pre)
+                src, pre = R(mx, 16 * q, 16 * q + 16), None
+            for q in range(ns, 2):
+                skip("v")
+        ts(R(mx, 48, 64), src, MAGIC, add, MAGIC, sub, soft=[sent])
+        tt(R(xw, 16, 32), src, R(mx, 48, 64), sub)
+        for (e, a, b) in cut["copy"]:
+            src = IX(window, R(offi, a // 16, b // 16))
+            if e == "a":
+                act(R(got, a, b), src, ACT.Identity, GATH)
+                tt(R(rr, a, b), R(got, a, b), bound(a, b, soft=[found]), ALU.max)
+            else:
+                tt(R(rr, a, b), src, R(bb, a, b), ALU.max, GATH)
+        for (_, a, b) in cut["bits"]:
+            ts(R(fb, a, b), R(rr, a, b), 0.0, ALU.max, KF - 63.5, add, 0.5)
+        for (_, a, b) in cut["code"]:
+            ka, kb = a // 16, b // 16
+            tk = token(kb - ka)
+            mm([[(PS(tk, 0, kb - ka), whole("id1"), R(lc, ka, kb))] + compact(tk, 0, "pf", fb, a, b)])
+            ts(R(offc, ka, kb), PS(tk, 0, kb - ka), 2.0, mul, -(KF / 128 + 1) * 4095 - 1, add)
+        for j, (e, a, b) in enumerate(cut["sum"]):
+            src, s_, r_ = IX(R(tab, 0, TW), R(offc, a // 16, b // 16)), R(ss, a, b), R(rr, a, b)
+            if e == "a":
+                act(s_, src, ACT.Identity, GATH)
+                op("g", DGE, lambda o=s_, i=r_: g.dma_start(ap(o), ap(i), accum_op=add), [r_, s_], [s_], dma="ad%d" % (4 * z + j),
+                   lat=DL + (b - a) * 512 / BW)
+            else:
+                tt(s_, src, r_, add, GATH)
+        for (e, a, b) in cut["floor"]:
+            if e == "a":
+                lin(R(nb, a, b), R(ss, a, b), -1.0, 127.5 - KN)
+            else:
+                ts(R(nb, a, b), R(ss, a, b), -1.0, mul, 127.5 - KN, add, 0.5)
+        nx, no = (yo, 0) if u == RU - 1 else ("xw%d%d" % (k, u + 1), W0)
+        for (_, a, b) in cut["out"]:
+            lin(R(nx, no + a, no + b), summed(a, b, [("id1", ss, 0), ("id1", nb, 0)]), 1.0, KN)
+            if u == RU - 1:
+                for (h, p0, p1) in halves:
+                    dma("s", T.y[64 * k:64 * k + 64, Q * h + a:Q * h + b], T[nx][p0:p1, a:b], [R(nx, a, b, p0, p1)], (), (b - a) * 256, sem="st")
 
-    for u in range(RU):
-        rule(u)
+    for stage in (setup, rule):
+        for u in range(RU):
+            for k in range(NS):
+                now[0] = k
+                stage(k, u)
     return ops
 
 
-def _arrange(ops, ref):
-    rest, pos, h = list(range(len(ref))), {}, 0
-    for s in ORDER:
-        if s > "f":
-            h = ord(s) - ord("g")
-        else:
-            i = rest.pop(32 * h + (ord(s) - ord("A") if s < "a" else ord(s) - ord("a") + 26))
-            pos[ref[i]["key"], ref[i]["u"]] = len(pos)
-            h = 0
-    at = []
-    for o in ops:
-        at.append(max([pos[o["key"], o["u"]]] + [at[d] + 1e-3 for d in o["deps"] | o["soft"]]))
-    loads = [i for i, o in enumerate(ops) if o["e"] == "s" and o["dma"] != "st"]
-    for i, p in zip(loads, sorted(at[i] for i in loads)):
-        at[i] = p - 1000
-    order = sorted(range(len(ops)), key=lambda i: (at[i], i))
-    fin, free, banks = {}, {}, [None] * 8
-    for i in order:
+def _graph(ops, pace):
+    pred = [sorted(o["deps"] | o["soft"]) for o in ops]
+    succ, gap = [[] for _ in ops], {}
+    for i, o in enumerate(ops):
+        for d in pred[i]:
+            succ[d].append(i)
+            gap[d, i] = ops[d]["lat"] + (pace[6] if ops[d]["e"] != o["e"] or ops[d]["dma"] else pace[7] * (d in o["deps"]))
+    return pred, succ, gap, pace[6]
+
+
+def _place(ops, graph, key, back):
+    pred, succ, gap = graph[:3]
+    up, down = (succ, pred) if back else (pred, succ)
+    left = [len(x) for x in up]
+    ready = [i for i in range(len(ops)) if not left[i]]
+    at, taken = [0.0] * len(ops), {e: [] for e in "vapgs"}
+    while ready:
+        i = min(ready, key=lambda j: key[j])
+        ready.remove(i)
+        c, row = ops[i]["c"], taken[ops[i]["e"]]
+        t = max([ops[i]["lat"] if back else 0.0] + [at[d] + ops[d]["c"] + (gap[i, d] if back else gap[d, i]) for d in up[i]])
+        k = len(row)
+        while k and row[k - 1][1] > t:
+            k -= 1
+        while k < len(row) and row[k][0] < t + c:
+            t = max(t, row[k][1])
+            k += 1
+        row.insert(k, (t, t + c))
+        at[i] = t
+        for j in down[i]:
+            left[j] -= 1
+            if not left[j]:
+                ready.append(j)
+    return at
+
+
+def _banks(ops, graph, at):
+    pred, _, gap, hop = graph
+    todo = sorted(range(len(ops)), key=lambda i: (at[i], i))
+    fin, free, held, order, start, bank = {}, {}, [None] * 8, [], [0.0] * len(ops), {}
+    while todo:
+        for x, i in enumerate(todo):
+            if not all(d in fin for d in pred[i]):
+                continue
+            tok = ops[i]["tok"]
+            if tok is None or tok["ops"][0] != i:
+                tok = None
+                break
+            since = [0.0 if not k else max(fin[j] for j in k["ops"]) if all(j in fin for j in k["ops"]) else None for k in held]
+            spare = [(max(since[b:b + tok["n"]]), b) for b in range(0, 9 - tok["n"], tok["n"]) if None not in since[b:b + tok["n"]]]
+            if spare:
+                break
+        todo.pop(x)
         o = ops[i]
-        t = max([free.get(o["e"], 0.0)] + [fin[d] + (LAT_X if ops[d]["e"] != o["e"] or ops[d]["dma"] else LAT_S * (d in o["deps"]))
-                                          for d in o["deps"] | o["soft"]])
-        tok = o["tok"]
-        if tok is not None and tok["b"] is None:
-            f, tok["b"] = min((max(fin[j] for j in k["ops"]) + LAT_X if k else 0.0, b) for b, k in enumerate(banks)
-                              if not k or all(j in fin for j in k["ops"]))
-            if banks[tok["b"]]:
-                o["deps"] |= {j for j in banks[tok["b"]]["ops"] if ops[j]["e"] != "p"}
-            banks[tok["b"]], t = tok, max(t, f)
-        free[o["e"]] = t + o["c"]
-        fin[i] = t + o["c"] + o["lat"]
-    return order, max(fin.values())
+        t = max([free.get(o["e"], 0.0)] + [fin[d] + gap[d, i] for d in pred[i]])
+        if tok is not None:
+            f, b = min(spare)
+            bank[i] = (b, {j for k in held[b:b + tok["n"]] if k for j in k["ops"] if ops[j]["e"] != "p"})
+            held[b:b + tok["n"]], t = [tok] * tok["n"], max(t, f + hop)
+        start[i], free[o["e"]] = t, t + o["c"]
+        fin[i] = t + o["c"]
+        order.append(i)
+    return max(fin[i] + ops[i]["lat"] for i in fin), order, start, bank
+
+
+def _replay(ops, graph, order, bank):
+    pred, _, gap, hop = graph
+    fin, free = [0.0] * len(ops), {e: 0.0 for e in "vapgs"}
+    for i in order:
+        t = max([free[ops[i]["e"]]] + [fin[d] + gap[d, i] for d in pred[i]] + [fin[d] + hop for d in (bank[i][1] if i in bank else ())])
+        free[ops[i]["e"]] = fin[i] = t + ops[i]["c"]
+    return max(fin[i] + ops[i]["lat"] for i in order)
+
+
+def _plan(progs, rounds):
+    ops, graphs = progs[0], [_graph(p, pace) for p, pace in zip(progs, PACES)]
+    n, graph, rng = len(ops), graphs[0], np.random.default_rng(SEED)
+    loads = [i for i in range(n) if (ops[i]["dma"] or "").startswith("dm")]
+
+    def tighten(key):
+        for back in (False, True, False):
+            for i in ([] if back else loads):
+                key[i] = i - 1e9
+            at = _place(ops, graph, key, back)
+            key = [-(at[i] + ops[i]["c"]) for i in range(n)]
+        end, order, start, bank = _banks(ops, graph, at)
+        ends = [end] + [_replay(p, q, order, bank) for p, q in zip(progs[1:], graphs[1:])]
+        return sum(e * PACES[0][0] / pace[0] for e, pace in zip(ends, PACES)) / len(PACES), ends, start
+    rest = [0.0] * n
+    for i in range(n - 1, -1, -1):
+        rest[i] = ops[i]["c"] + max([ops[i]["lat"]] + [graph[2][i, j] + rest[j] for j in graph[1][i]])
+    best = now = tighten([-rest[i] - (LEAD if ops[i]["s"] == 0 else 0.0) for i in range(n)])
+    for r in range(rounds):
+        shake = rng.normal(0.0, rng.choice([100.0, 300.0, 800.0]), n) * (rng.random(n) < 0.3)
+        new = tighten([float(t) for t in np.array(now[2]) + shake])
+        if new[0] < now[0] + 100.0 * (1 - r / rounds):
+            now = new
+        if new[0] < best[0]:
+            best = new
+    return best
+
+
+PLAN = {}
+
+
+def _arrange(ops, at):
+    end, order, start, bank = _banks(ops, _graph(ops, PACES[0]), at)
+    for i, (b, waits) in bank.items():
+        ops[i]["tok"]["b"] = b
+        ops[i]["deps"] |= waits
+    return order, end, start
 
 
 def rank_program(g, core, T, topo):
     rank = T.rank_of(core)
     if rank is None:
         return
-    ops = _program(g, T, topo, rank)
-    order = _arrange(ops, _program(g, T, topo, HB))[0]
+    ops = _program(g, T, topo, rank, PACES[0])
+    if not PLAN:
+        PLAN["at"] = _plan([_program(g, T, topo, HB, pace) for pace in PACES], ROUNDS)[2]
+    order = _arrange(ops, PLAN["at"])[0]
     queue = {"v": g.vector, "a": g.scalar, "p": g.tensor, "g": g, "s": g.sync}
     needed = set().union(*[o["deps"] for o in ops])
     mark, total, clock, known = {}, {}, {}, {e: {} for e in queue}
     place = {i: p for p, i in enumerate(order)}
     for i in order:
         o = ops[i]
+        if o["fn"] is None:
+            continue
         q, kn = queue[o["e"]], known[o["e"]]
         for d in sorted(o["deps"], key=lambda d: -place[d]):
             s, v = mark[d]
@@ -414,7 +566,7 @@ def rank_program(g, core, T, topo):
             total[s] = total.get(s, 0) + (16 if o["dma"] else 1)
             mark[i], clock[i] = (s, total[s]), dict(kn)
             ins.then_inc(T.sem[s], 16 if o["dma"] else 1)
-    sent = ENG_PER_DST * RU * min(HB, len(T.cores) - 1 - rank)
+    sent = ENG_PER_DST * RU * NS * min(HB, len(T.cores) - 1 - rank)
     if sent:
         g.wait_ge(T.sem.loc, sent)
     for s in sorted(total, key=lambda s: s == "st"):

@@ -3,17 +3,22 @@ from concourse.bass import DstId, RemoteDMATransfer
 from concourse.mybir import AluOpType as ALU, ActivationFunctionType as ACT, AxisListType as AX
 
 P, Q, W0, RU, HB, TW, NS, BANK = 3072, 1536, 32, 3, 3, 4096, 2, 512
-CUT = {"sign": "384 384 384 384", "scan": "768 768", "sel": "a480 a480 v576", "find": "1536", "low": "a256 a512 a512 a256",
+CUT = {"sign": "384 384 384 384", "scan": "768 768", "sel": "a384 a384 v384 v384", "find": "1536", "low": "a768 a768",
        "copy": "v384 a384 a384 a384", "bits": "768 768", "code": "768 768", "sum": "384 384 384 384", "floor": "a384 a384 a384 v384",
        "out": "384 384 384 384"}
-LAST = {}
+LAST = {"floor": "a384 a384 a384 a384", "out": "a384 a384 a384 v384"}
 KF, KN, NC, MAGIC, EVEN = 24576.0, 49152.0, -384.0, 1.5 * 2.0 ** 33, 1.5 * 2.0 ** 24
-ENG_PER_DST = 4
-PACES = [(0.95, 0.5, 1.45, 4000.0, 57.0, 75.0, 160.0, 85.0), (0.83, 0.415, 1.56, 3700.0, 50.0, 65.0, 150.0, 80.0),
-         (0.83, 0.45, 1.1, 4500.0, 50.0, 65.0, 200.0, 100.0), (1.2, 0.7, 1.7, 3500.0, 72.0, 95.0, 150.0, 80.0)]
+PACES = [(1.1, 0.71, 1.55, 4000.0, 66.0, 92.0, 340.0, 180.0), (0.95, 0.55, 1.4, 3600.0, 57.0, 75.0, 260.0, 140.0),
+         (1.1, 0.6, 1.55, 4200.0, 66.0, 88.0, 420.0, 220.0), (1.2, 0.64, 1.9, 4200.0, 72.0, 120.0, 300.0, 160.0),
+         (1.2, 0.84, 1.6, 4000.0, 72.0, 96.0, 320.0, 170.0)]
 LEAD, OM, DL, BW, DGE = 3000.0, 3.0, 1300.0, 280.0, 1000.0
-ROUNDS, SEED = 1200, 1
-LOC = "vv"
+ROUNDS, SEED = 6500, 1
+LOC, GEN, FOLD, FX = "avv", "gaaggvv", True, -200.0
+FIRST = {}
+LOAD = ["512 1024", "1536"]
+LCPRE = True
+EARLY = 1536
+ROW, RAMP = True, 384
 
 
 def _scratch():
@@ -40,23 +45,22 @@ def _scratch():
         add("mx" + n, 72, "float32")
         add("lc" + n, 96, "float16")
     add("ramp", Q, "float16")
-    add("ones", BANK, "float16")
-    add("jr", 144, "float32")
+    add("ones", BANK, "bfloat16")
     add("vk pp id1 ida idv", 128, "bfloat16")
     add("vs as", 72, "bfloat16")
     add("gcol msk", 256, "bfloat16")
     add("fm sm", 256, "float16")
-    add("pf em", 144, "bfloat16")
+    add("pf pl em", 144, "bfloat16")
     add("kz", 112, "bfloat16")
     add("pi", 8, "int32")
-    add("col q16 cw ck hls bz", 16, "float32")
+    add("col q16 cw ck hls bz tag", 16, "float32")
     add("wk", 8, "bfloat16")
     s["ps"] = ("psum", [128, 8 * BANK], "float32")
     return s
 
 
 SCRATCH = _scratch()
-SEMAPHORES = ["ev", "ea", "ep", "eg", "loc", "st"] + ["arr%d" % i for i in range(NS * RU)] + ["dm%d" % i for i in range(24)] + ["ad%d" % i for i in range(24)]
+SEMAPHORES = ["ev", "ea", "ep", "eg", "loc", "st", "tb0", "tb1", "ta0", "ta1", "row"] + ["arr%d" % i for i in range(NS * RU)] + ["dm%d" % i for i in range(24)]
 ENGSEM = {"v": "ev", "a": "ea", "p": "ep", "g": "eg"}
 
 
@@ -71,6 +75,10 @@ def _cuts(text):
 
 def _banked(a, b):
     return [(c - a, c, min(c + BANK, b)) for c in range(a, b, BANK)]
+
+
+def _lanes(T, topo, rank):
+    return len(topo.engines(T.cores[rank], T.cores[rank + 1]))
 
 
 def R(b, lo, hi, p0=0, p1=128, st=1):
@@ -150,22 +158,25 @@ def _program(g, T, topo, rank, pace):
         return act(out, in_, ACT.Identity, scale=scale, bias=bias)
 
     def fill(out, val):
-        return lin(out, R("vk", 0, out[3] - out[2], out[4], out[5]), 0.0, val)
+        return lin(out, R("gcol", 0, out[3] - out[2], out[4], out[5]), 0.0, val)
 
     def copy(eng, out, in_):
+        if eng == "g":
+            n = out[3] - out[2]
+            return op("g", 200.0 + 2 * CYC * n, lambda: g.affine_select(ap(out), ap(in_), [[0, n]], ALU.is_ge, 0.0, 0, 0), [in_], [out])
         return act(out, in_, ACT.Identity) if eng == "a" else call("v", 1.0, V.tensor_copy, out, [in_])
 
     def skip(eng, soft=()):
         return op(eng, 0.0, None, soft=soft)
 
-    def mm(groups, **k):
+    def mm(groups, start=True, stop=True, **k):
         items = [it for grp in groups for it in grp]
         cost = sum(max(64, (it[0][3] - it[0][2] + it[0][6] - 1) // it[0][6]) for it in items) * PCY + 20.0 + OM * len(items)
 
         def fn():
             for grp in groups:
                 for q, (o, lhs, rhs) in enumerate(grp):
-                    last = PE.matmul(ap(o), ap(lhs), ap(rhs), q == 0, q == len(grp) - 1)
+                    last = PE.matmul(ap(o), ap(lhs), ap(rhs), start and q == 0, stop and q == len(grp) - 1)
             return last
         return op("p", cost, fn, [x for it in items for x in it[1:]], (), tok=items[0][0][1], **k)
 
@@ -180,6 +191,9 @@ def _program(g, T, topo, rank, pace):
     def iota(out, pattern, base, cm=0):
         kw = {} if out[1] == "pi" else {"allow_small_or_imprecise_dtypes": True}
         return op("g", 160.0 + 2 * CYC * (out[3] - out[2]), lambda: g.iota(ap(out), pattern, base, cm, **kw), (), [out])
+
+    def keep(out, in_, pattern, cmp, base, cm):
+        return op("g", 200.0 + 2 * CYC * (out[3] - out[2]), lambda: g.affine_select(ap(out), ap(in_), pattern, cmp, 0.0, base, cm), [in_], [out])
 
     def dma(eng, out, in_, rd, wr, nbytes, sem=None):
         if sem is None:
@@ -196,7 +210,7 @@ def _program(g, T, topo, rank, pace):
 
     add, mul, eq, sub = ALU.add, ALU.mult, ALU.is_equal, ALU.subtract
     halves = [(h, 64 * h, 64 * h + 64) for h in range(2)]
-    first = [_cuts("512 1024"), _cuts("1536")]
+    first = [_cuts(x) for x in LOAD]
 
     dma("a", T.wk[:, 3:6], T.kc[:, :], (), [R("wk", 3, 6)], 0)
     dma("a", T.wk[:, 0:3], T.wa[:, :], (), [R("wk", 0, 3)], 0)
@@ -211,22 +225,32 @@ def _program(g, T, topo, rank, pace):
                 done += (b - a) * 128
                 dma("s", T["xw%d0" % k][p0:p1, W0 + a:W0 + b], T.x[64 * k:64 * k + 64, Q * h + a:Q * h + b], (),
                     [R("xw%d0" % k, W0 + a, W0 + b, p0, p1)], done)
-    for k in range(NS):
-        for (h, p0, p1) in halves:
-            done += TW * 128
-            dma("s", T["tab%d" % k][p0:p1, :], T.inv[64 * k:64 * k + 64, :], (), [R("tab%d" % k, 0, TW, p0, p1)], done)
 
-    jr = R("jr", 0, 144)
+    def table(k, done, after, sems, soft=()):
+        for (h, p0, p1) in halves:
+            i = dma("s", T["tab%d" % k][p0:p1, :], T.inv[64 * k:64 * k + 64, :], after, [R("tab%d" % k, 0, TW, p0, p1)], done + TW * 128 * (h + 1), sems[h])
+            ops[i]["soft"] |= set(soft)
+    if not ROW:
+        table(0, done, (), (None, None))
+
     iota(R("pi", 0, 1), [[0, 1]], 0, 1)
-    for j in range(4):
-        iota(R("vk", 32 * j, 32 * j + 32), [[1, 16], [-1, 2]], 16 << j)
     iota(R("vs", 0, 64), [[0, 2], [1, 16], [-1, 2]], 0)
-    iota(R("vs", 64, 66), [[0, 2]], -5)
-    for e in range(2):
-        iota(R("gcol", 128 * e, 128 * e + 128), [[2, 2], [4, 4], [0, 16]], e)
+    for j in range(4):
+        if GEN[0] == "g":
+            iota(R("vk", 32 * j, 32 * j + 32), [[1, 16], [-1, 2]], 16 << j)
+        else:
+            lin(R("vk", 32 * j, 32 * j + 32), R("vs", 0, 32), 1.0, float(16 << j))
+    if GEN[1] == "g":
+        iota(R("vs", 64, 66), [[0, 2]], -5)
+    else:
+        lin(R("vs", 64, 66), R("vs", 0, 2), 0.0, -5.0)
+    iota(R("gcol", 0, 128), [[2, 2], [4, 4], [0, 16]], 0)
+    if GEN[2] == "g":
+        iota(R("gcol", 128, 256), [[2, 2], [4, 4], [0, 16]], 1)
+    else:
+        lin(R("gcol", 128, 256), R("gcol", 0, 128), 1.0, 1.0)
     for j in (3, 2, 1, 0):
         iota(R("pp", 0, 128, 0, 16 * j + 16), [[0, 64 >> j], [4096, 2], [0, 1 << j]], -2048)
-    iota(jr, [[1, 144]], 0)
     ts(R("pi", 1, 2), R("pi", 0, 1), 15, ALU.bitwise_and)
     ts(R("pi", 2, 3), R("pi", 0, 1), 2, ALU.logical_shift_right, 12, ALU.bitwise_and)
     ts(R("pi", 3, 4), R("pi", 0, 1), 5, ALU.logical_shift_right, 2, ALU.bitwise_and)
@@ -246,33 +270,56 @@ def _program(g, T, topo, rank, pace):
     ts(R("msk", 0, 256, 0, 64), R("gcol", 0, 256, 0, 64), col(1, 0, 64), eq, f=0.5)
     for e in range(2):
         tt(R("fm", 128 * e, 128 * e + 128, 0, 64), R("msk", 128 * e, 128 * e + 128, 0, 64), R("pp", 0, 128, 0, 64), mul)
-    copy("a", R("sm", 0, 256, 0, 64), R("fm", 0, 256, 0, 64))
+    copy(GEN[3], R("sm", 0, 256, 0, 64), R("fm", 0, 256, 0, 64))
     ts(R("fm", 0, 256, 64, 96), R("gcol", 0, 256, 64, 96), col(1, 64, 96), eq, col(8, 64, 96), mul, 0.5)
     ts(R("sm", 0, 256, 64, 96), R("gcol", 0, 256, 64, 96), col(1, 64, 96), eq, col(9, 64, 96), mul, 0.5)
     mset(R("fm", 0, 256, 96, 98), 1.0)
     fill(R("fm", 0, 128, 96, 97), 2046.0)
     fill(R("fm", 128, 256, 96, 97), 2048.0)
     mset(R("sm", 0, 256, 96, 97), -8192.0)
-    mset(R("ones", 0, BANK), 1.0)
-    for (_, a, b) in _banked(0, Q):
-        call("v", 0.5, V.tensor_tensor_scan, R("ramp", a, b), [R("ones", 0, BANK), R("ones", 0, BANK), 2.0 * a - 1521.0], [add, add])
+    mset(R("ones", 0, RAMP), 1.0)
+    call("v", 0.5, V.tensor_tensor_scan, R("ramp", 0, RAMP), [R("ones", 0, RAMP), R("ones", 0, RAMP), -1521.0], [add, add])
+    a = RAMP
+    while a < Q:
+        b = min(2 * a, Q)
+        if GEN[5] == "a":
+            lin(R("ramp", a, b), R("ramp", 0, b - a), 1.0, 2.0 * a)
+        else:
+            ts(R("ramp", a, b), R("ramp", 0, b - a), 2.0 * a, add, f=0.5)
+        a = b
     for k in range(NS):
         now[0] = k
-        for (_, a, b) in first[k]:
-            ts(R("tile%d" % k, a // 2, b // 2, 96, 98), R("ramp", a, b, 96, 98, 2), 1.0, add, f=0.5)
+        if k and ROW:
+            row = dma("s", T.tile1[97:98, :], T.tile0[97:98, :], [R("tile0", 0, Q // 2, 97, 98)], [R("tile1", 0, Q // 2, 97, 98)], 0, "row")
+            table(0, 0, (), ("ta0", "ta1"), [row])
+        else:
+            for (_, a, b) in _cuts("768 768"):
+                if GEN[6] == "a":
+                    lin(R("tile%d" % k, a // 2, b // 2, 96, 98), R("ramp", a, b, 96, 98, 2), 1.0, 1.0)
+                else:
+                    ts(R("tile%d" % k, a // 2, b // 2, 96, 98), R("ramp", a, b, 96, 98, 2), 1.0, add, f=0.5)
         lin(R("dd%d" % k, 0, 1), col(1), 2.0, 32.0 - 1584.0)
     now[0] = 0
-    ts(col(4), col(0), col(1), sub, 15.0, add)
-    lin(col(6), col(3), 512.0, 1024.0 * (2 * rank + 1))
-    ts(R("em", 0, 144), jr, col(4), eq)
-    ts(whole("id1"), whole("jr"), col(0), eq)
-    ts(R("q16", 0, 16), R("jr", 0, 16), col(1), ALU.is_lt, 1.0, add)
+    for (h, p0, p1) in halves[::-1]:
+        iota(R("tag", 0, 1, 0, p1), [[0, 1]], 1024 * (2 * rank + 1 + h))
+    em = R("em", 0, 144)
+    keep(whole("id1"), whole("ones"), [[-1, 128]], eq, 0, 1)
+    keep(em, R("ones", 0, 144), [[0, 9], [1, 16]], eq, -15, 0)
+    keep(em, em, [[-1, 144]], ALU.is_ge, 15, 1)
+    keep(em, em, [[1, 144]], ALU.is_ge, 0, -1)
+    ts(R("q16", 0, 16), R("vs", 0, 32, st=2), col(1), ALU.is_lt, 1.0, add)
     call("v", 1.0, V.tensor_reduce, col(11), [R("q16", 0, 16)], [AX.X, mul])
     ts(col(12), col(1), 12.0, ALU.is_lt, 1.0 / 256, mul)
     ts(R("pf", 0, 144), R("em", 0, 144), col(11), mul, col(12), mul, 0.5)
+    if not LCPRE:
+        lin(R("pl", 0, 144), R("pf", 0, 144), -128.0, 0.0)
     for (e, v) in (("a", 256.0), ("v", 512.0)):
-        if e in CUT["low"] + LAST.get("low", ""):
-            lin(whole("id" + e), whole("id1"), v, 0.0)
+        if e in CUT["low"] + LAST.get("low", "") + FIRST.get("low", ""):
+            if GEN[4] == "a":
+                lin(whole("id" + e), whole("id1"), v, 0.0)
+            else:
+                iota(whole("id" + e), [[0, 128]], int(v))
+                keep(whole("id" + e), whole("id" + e), [[-1, 128]], eq, 0, 1)
     for (e, v) in (("a", -1600), ("v", 100352)):
         mine = [c for c in _cuts(CUT["sel"]) if c[0] == e]
         if mine:
@@ -282,12 +329,18 @@ def _program(g, T, topo, rank, pace):
         n = "%d%d" % (k, u)
         ts(R("lt" + n, 0, 128), whole("vk"), col(4 * k + u, b="ck"), eq, f=0.5)
         lin(R("lt" + n, 128, 194), R("as", 0, 66), col(8 * k + u, b="cw"), 0.0)
-        iota(R("xw" + n, 0, 32), [[-32384, 2], [0, 16]], int(NC))
+        if u > 0 and EARLY < Q:
+            tk = token(1)
+            mm([[(PS(tk, 0, 1, 0, 97), R("lt" + n, e, 194, st=2), R("ones", 0, 1)) for e in range(2)]])
+            lin(col(3 * k + u + 8, 0, 97, "bz"), PS(tk, 0, 1, 0, 97), KN, col(3 * k + u, 0, 97, "bz"))
+        if FOLD:
+            iota(R("cb" + n, 0, 16), [[0, 16]], int(NC))
+        iota(R("xw" + n, 0, 32), [[-16384, 2], [0, 16]], int(NC))
         iota(R("land" + n, 48, 64, 0, 64), [[0, 16]], int(NC))
 
     def rule(k, u):
         n, z = "%d%d" % (k, u), NS * u + k
-        cut = {x: _cuts(LAST.get(x, y) if u == RU - 1 else y) for x, y in CUT.items()}
+        cut = {x: _cuts({0: FIRST, RU - 1: LAST}.get(u, {}).get(x, y)) for x, y in CUT.items()}
         xw, tile, dd = "xw" + n, "tile%d" % k, "dd%d" % k
         lo, fb, nb, yo, got, sel, rr, ss, bb, tab, offi, offc, ia, ib, mx, lc = [
             "%s%d" % (x, k) for x in "lo fb nb yo got sel rr ss bb tab offi offc ia ib mx lc".split()]
@@ -298,9 +351,11 @@ def _program(g, T, topo, rank, pace):
         for (_, a, b) in cut["sign"]:
             w = (b - a) // 2
             tk = token(w)
-            mm([[(PS(tk, c, c + y - x, 0, 97), R("lt" + n, e, 194, st=2), R(xw, W0 + 2 * x + e, W0 + 2 * y, st=2)) for e in range(2)]
+            early = u > 0 and a >= EARLY
+            parts = [(ss, 0), (nb, 0)] if early else [(xw, W0)]
+            mm([[(PS(tk, c, c + y - x, 0, 97), R("lt" + n, e, 194, st=2), R(src, c0 + 2 * x + e, c0 + 2 * y, st=2)) for (src, c0) in parts for e in range(2)]
                 for (c, x, y) in _banked(a // 2, b // 2)])
-            act(R(tile, a // 2, b // 2, 0, 97), PS(tk, 0, w, 0, 97), ACT.Sign, bias=col(3 * k + u, 0, 97, "bz"))
+            act(R(tile, a // 2, b // 2, 0, 97), PS(tk, 0, w, 0, 97), ACT.Sign, bias=col(3 * k + u + 8 * early, 0, 97, "bz"))
         for (_, a, b) in cut["scan"]:
             tk = token(b - a)
             mm([[m] for run in _banked(a, b) for m in form(tk, "fm", 98, *run)])
@@ -325,25 +380,28 @@ def _program(g, T, topo, rank, pace):
             ts(R(ib, ka, kb), R(ia, ka, kb), 4095, ALU.bitwise_and)
             found = ts(R(offi, ka, kb), R(ib, ka, kb), -1.0, mul, 1600.0, add)
         sm, cb, land = "sm" + n, "cb" + n, "land" + n
-        sent = ts(R(sm, 0, 16), IX(window, R(offi, 96, 97)), col(6), add, NC, ALU.max)
+        if LOC[2] == "a":
+            sent = lin(R(sm, 0, 16), IX(window, R(offi, 96, 97)), 1.0, col(0, b="tag"))
+        else:
+            sent = ts(R(sm, 0, 16), IX(window, R(offi, 96, 97)), col(0, b="tag"), add)
         copy(LOC[0], R(land, 48, 64, 64, 128), R(sm, 0, 16, 0, 64))
         dsts = [rank + d for d in range(1, HB + 1) if rank + d < len(T.cores)]
-        if dsts:
+        srcs = [R(sm, 0, 16), R(cb, 0, 16), R(land, 48, 64)] if FOLD else [R(cb, 0, 16)]
+        if not dsts:
+            for e in (LOC[1] if FOLD else "v" + LOC[1]):
+                skip(e)
+        elif FOLD:
+            copy(LOC[1], R(cb, 0, 16, 0, 64), R(sm, 0, 16, 64, 128))
+        else:
             tt(R(cb, 0, 16, 64, 128), R(sm, 0, 16, 64, 128), R(land, 48, 64, 64, 128), ALU.max)
             copy(LOC[1], R(cb, 0, 16, 0, 64), R(cb, 0, 16, 64, 128))
-        else:
-            skip("v")
-            skip(LOC[1])
 
         def send():
-            trs = []
-            for q, r2 in enumerate(dsts):
-                rid, pid = topo.addr(T.cores[r2])[:2]
-                eng = topo.engines(T.cores[rank], T.cores[r2])[q * ENG_PER_DST:(q + 1) * ENG_PER_DST]
-                trs.append(RemoteDMATransfer(dst_ids=[DstId(rid=rid, pnc=pid)], dma_engine_mask=sum(1 << e for e in eng),
-                                             remote_sem=T.sem["arr%d" % z], src=ap(R(cb, 0, 16)), dst=ap(R(land, 16 * q, 16 * q + 16))))
-            g.remote_dma_fused(trs, local_sem=T.sem.loc)
-        sent = op("g", 1000.0, send if dsts else None, [R(cb, 0, 16)] if dsts else (), (), soft=[sent], lat=XCH - 1000.0)
+            ids = [DstId(rid=topo.addr(T.cores[r2])[0], pnc=topo.addr(T.cores[r2])[1]) for r2 in dsts]
+            g.remote_dma_fused([RemoteDMATransfer(dst_ids=ids, dma_engine_mask=topo.mask(T.cores[rank], T.cores[dsts[0]]), remote_sem=T.sem["arr%d" % z],
+                                                  srcs=[ap(x) for x in srcs], dsts=[ap(R(land, 16 * q, 16 * q + 16)) for q in range(len(dsts))],
+                                                  alu_op=2 if FOLD else 0)], local_sem=T.sem.loc)
+        sent = op("g", 1000.0, send if dsts else None, srcs if dsts else (), (), soft=[sent], lat=XCH - 1000.0 + FOLD * FX)
 
         def bound(a, b, **k2):
             e = [c[0] for c in cut["low"] if c[1] <= a < c[2]][0]
@@ -361,12 +419,12 @@ def _program(g, T, topo, rank, pace):
         for (e, a, b) in cut["copy"]:
             if e == "v":
                 copy("a", R(bb, a, b), bound(a, b))
-        for (e, a, b) in runs:
+        for (e, a, b) in (runs if LCPRE else []):
             tk = token((b - a) // 16)
             mm([compact(tk, 0, "pf", lo, a, b)])
             lin(R(lc, a // 16, b // 16), PS(tk, 0, (b - a) // 16), -128.0 if e == "a" else -256.0, 0.5)
         ns = min(rank, HB)
-        pre, src = (("arr%d" % z, ENG_PER_DST * ns) if ns else None), R(land, 48, 64)
+        pre, src = (("arr%d" % z, sum(_lanes(T, topo, rank - q) for q in range(1, ns + 1))) if ns else None), R(land, 48, 64)
         if ns == 3:
             tt(R(mx, 0, 32), R(land, 0, 32), R(land, 32, 64), ALU.max, soft=[sent], pre=pre)
             tt(R(mx, 32, 48), R(mx, 0, 16), R(mx, 16, 32), ALU.max)
@@ -386,29 +444,42 @@ def _program(g, T, topo, rank, pace):
                 tt(R(rr, a, b), R(got, a, b), bound(a, b, soft=[found]), ALU.max)
             else:
                 tt(R(rr, a, b), src, R(bb, a, b), ALU.max, GATH)
+        if z == 0:
+            table(1, 0, [R(rr, 0, 16)], ("tb0", "tb1"))
         for (_, a, b) in cut["bits"]:
             ts(R(fb, a, b), R(rr, a, b), 0.0, ALU.max, KF - 63.5, add, 0.5)
         for (_, a, b) in cut["code"]:
             ka, kb = a // 16, b // 16
             tk = token(kb - ka)
-            mm([[(PS(tk, 0, kb - ka), whole("id1"), R(lc, ka, kb))] + compact(tk, 0, "pf", fb, a, b)])
-            ts(R(offc, ka, kb), PS(tk, 0, kb - ka), 2.0, mul, -(KF / 128 + 1) * 4095 - 1, add)
+            if LCPRE:
+                mm([[(PS(tk, 0, kb - ka), whole("id1"), R(lc, ka, kb))] + compact(tk, 0, "pf", fb, a, b)])
+            else:
+                mm([compact(tk, 0, "pl", lo, a, b)], stop=False, soft=[h[0] for h in hist[rr] if h[2] and h[1][2] <= a < h[1][3]])
+                mm([compact(tk, 0, "pf", fb, a, b)], start=False)
+            ts(R(offc, ka, kb), PS(tk, 0, kb - ka), 2.0, mul, -(KF / 128 + 1) * 4095 - LCPRE, add)
         for j, (e, a, b) in enumerate(cut["sum"]):
-            src, s_, r_ = IX(R(tab, 0, TW), R(offc, a // 16, b // 16)), R(ss, a, b), R(rr, a, b)
+            src = IX(R(tab, 0, TW), R(offc, a // 16, b // 16))
             if e == "a":
-                act(s_, src, ACT.Identity, GATH)
-                op("g", DGE, lambda o=s_, i=r_: g.dma_start(ap(o), ap(i), accum_op=add), [r_, s_], [s_], dma="ad%d" % (4 * z + j),
-                   lat=DL + (b - a) * 512 / BW)
+                act(R(ss, a, b), src, ACT.Identity, GATH)
             else:
-                tt(s_, src, r_, add, GATH)
+                tt(R(ss, a, b), src, R(rr, a, b), add, GATH)
+
+        def terms(a):
+            return [("id1", ss, 0)] + [("id1", rr, 0) for c in cut["sum"] if c[0] == "a" and c[1] <= a < c[2]]
         for (e, a, b) in cut["floor"]:
+            two = len(terms(a)) == 2
+            src = summed(a, b, terms(a)) if two else R(ss, a, b)
             if e == "a":
-                lin(R(nb, a, b), R(ss, a, b), -1.0, 127.5 - KN)
+                lin(R(nb, a, b), src, -1.0, 127.5 - KN)
             else:
-                ts(R(nb, a, b), R(ss, a, b), -1.0, mul, 127.5 - KN, add, 0.5)
+                ts(R(nb, a, b), src, -1.0, mul, 127.5 - KN, add, 1.0 if two else 0.5)
         nx, no = (yo, 0) if u == RU - 1 else ("xw%d%d" % (k, u + 1), W0)
-        for (_, a, b) in cut["out"]:
-            lin(R(nx, no + a, no + b), summed(a, b, [("id1", ss, 0), ("id1", nb, 0)]), 1.0, KN)
+        for (e, a, b) in cut["out"]:
+            src = summed(a, b, terms(a) + [("id1", nb, 0)])
+            if e == "v":
+                ts(R(nx, no + a, no + b), src, KN, add)
+            else:
+                lin(R(nx, no + a, no + b), src, 1.0, KN)
             if u == RU - 1:
                 for (h, p0, p1) in halves:
                     dma("s", T.y[64 * k:64 * k + 64, Q * h + a:Q * h + b], T[nx][p0:p1, a:b], [R(nx, a, b, p0, p1)], (), (b - a) * 256, sem="st")
@@ -500,23 +571,30 @@ def _plan(progs, rounds):
     n, graph, rng = len(ops), graphs[0], np.random.default_rng(SEED)
     loads = [i for i in range(n) if (ops[i]["dma"] or "").startswith("dm")]
 
-    def tighten(key):
-        for back in (False, True, False):
+    def tighten(key, passes=(False, True, False), limit=1e9):
+        for back in passes:
             for i in ([] if back else loads):
                 key[i] = i - 1e9
             at = _place(ops, graph, key, back)
             key = [-(at[i] + ops[i]["c"]) for i in range(n)]
         end, order, start, bank = _banks(ops, graph, at)
+        if end > limit:
+            return (1e9,)
         ends = [end] + [_replay(p, q, order, bank) for p, q in zip(progs[1:], graphs[1:])]
         return sum(e * PACES[0][0] / pace[0] for e, pace in zip(ends, PACES)) / len(PACES), ends, start
-    rest = [0.0] * n
+    rest, stream = [0.0] * n, np.array([o["s"] for o in ops])
     for i in range(n - 1, -1, -1):
         rest[i] = ops[i]["c"] + max([ops[i]["lat"]] + [graph[2][i, j] + rest[j] for j in graph[1][i]])
     best = now = tighten([-rest[i] - (LEAD if ops[i]["s"] == 0 else 0.0) for i in range(n)])
     for r in range(rounds):
-        shake = rng.normal(0.0, rng.choice([100.0, 300.0, 800.0]), n) * (rng.random(n) < 0.3)
-        new = tighten([float(t) for t in np.array(now[2]) + shake])
-        if new[0] < now[0] + 100.0 * (1 - r / rounds):
+        at = np.array(now[2])
+        near = abs(at - rng.random() * at.max()) < rng.choice([1500.0, 3000.0, 6000.0])
+        if rng.random() < 0.3:
+            shake = rng.normal(0.0, 1500.0) * (stream == rng.integers(NS))
+        else:
+            shake = rng.normal(0.0, rng.choice([200.0, 500.0, 1200.0]), n) * (rng.random(n) < 0.5)
+        new = tighten([float(t) for t in at + shake * near], (False, True, False)[:rng.choice([1, 3])], now[1][0] + 400.0)
+        if new[0] < now[0] - 15.0 * (1 - r / rounds) * np.log(rng.random()):
             now = new
         if new[0] < best[0]:
             best = new
@@ -566,8 +644,7 @@ def rank_program(g, core, T, topo):
             total[s] = total.get(s, 0) + (16 if o["dma"] else 1)
             mark[i], clock[i] = (s, total[s]), dict(kn)
             ins.then_inc(T.sem[s], 16 if o["dma"] else 1)
-    sent = ENG_PER_DST * RU * NS * min(HB, len(T.cores) - 1 - rank)
-    if sent:
-        g.wait_ge(T.sem.loc, sent)
+    if rank + 1 < len(T.cores):
+        g.wait_ge(T.sem.loc, RU * NS * _lanes(T, topo, rank))
     for s in sorted(total, key=lambda s: s == "st"):
         g.wait_ge(T.sem[s], total[s])

import numpy as np
from concourse.bass import DstId, RemoteDMATransfer
from concourse.mybir import AluOpType as ALU, ActivationFunctionType as ACT, AxisListType as AX

P, Q, W0, RU, HB, TW, NS, BANK = 3072, 1536, 32, 3, 3, 4096, 2, 512
CUT = {"sign": "384 384 384 384", "scan": "768 768", "sel": "a384 a384 v384 v384", "find": "1536", "low": "a768 a768",
       "copy": "v384 a384 a384 a384", "bits": "768 768", "code": "768 768", "sum": "384 384 384 384", "floor": "a384 a384 a384 v384",
       "out": "384 384 384 384"}
LAST = {"floor": "a384 a384 a384 a384", "out": "a384 a384 a384 v384"}
KF, KN, NC, MAGIC, EVEN = 24576.0, 49152.0, -384.0, 1.5 * 2.0 ** 33, 1.5 * 2.0 ** 24
PACES = [(1.1, 0.71, 1.55, 4000.0, 66.0, 92.0, 340.0, 180.0), (0.95, 0.55, 1.4, 3600.0, 57.0, 75.0, 260.0, 140.0),
         (1.1, 0.6, 1.55, 4200.0, 66.0, 88.0, 420.0, 220.0), (1.2, 0.64, 1.9, 4200.0, 72.0, 120.0, 300.0, 160.0),
         (1.2, 0.84, 1.6, 4000.0, 72.0, 96.0, 320.0, 170.0)]
LEAD, OM, DL, BW, DGE = 3000.0, 3.0, 1300.0, 280.0, 1000.0
ROUNDS, SEED = 6500, 1
LOC, GEN, FOLD, FX = "avv", "gaaggvv", True, -200.0
FIRST = {}
LOAD = ["512 1024", "1536"]
LCPRE = True
EARLY = 1536
ROW, RAMP = True, 384


def _scratch():
    s = {}

    def add(names, n, dt):
        for x in names.split():
            s[x] = ("sbuf", [128, n], dt)
    for k in range(NS):
        for u in range(RU):
            n = "%d%d" % (k, u)
            add("xw" + n, W0 + Q, "bfloat16")
            add("lt" + n, 200, "bfloat16")
            add("sm%s cb%s" % (n, n), 16, "float32")
            add("land" + n, 64, "float32")
        n = "%d" % k
        add(" ".join(x + n for x in "lo fb nb yo got".split()), Q, "bfloat16")
        add(" ".join(x + n for x in "sel rr ss bb".split()), Q, "float16")
        add("dd" + n, Q + 16, "float16")
        add("tile" + n, Q // 2, "float16")
        add("tab" + n, TW, "bfloat16")
        add("offi%s offc%s" % (n, n), 112, "uint16")
        add("ia%s ib%s" % (n, n), 112, "int32")
        add("mx" + n, 72, "float32")
        add("lc" + n, 96, "float16")
    add("ramp", Q, "float16")
    add("ones", BANK, "bfloat16")
    add("vk pp id1 ida idv", 128, "bfloat16")
    add("vs as", 72, "bfloat16")
    add("gcol msk", 256, "bfloat16")
    add("fm sm", 256, "float16")
    add("pf pl em", 144, "bfloat16")
    add("kz", 112, "bfloat16")
    add("pi", 8, "int32")
    add("col q16 cw ck hls bz tag", 16, "float32")
    add("wk", 8, "bfloat16")
    s["ps"] = ("psum", [128, 8 * BANK], "float32")
    return s


SCRATCH = _scratch()
SEMAPHORES = ["ev", "ea", "ep", "eg", "loc", "st", "tb0", "tb1", "ta0", "ta1", "row"] + ["arr%d" % i for i in range(NS * RU)] + ["dm%d" % i for i in range(24)]
ENGSEM = {"v": "ev", "a": "ea", "p": "ep", "g": "eg"}


def _cuts(text):
    out, a = [], 0
    for x in text.split():
        n = int(x.lstrip("av"))
        out.append((x[0], a, a + n))
        a += n
    return out


def _banked(a, b):
    return [(c - a, c, min(c + BANK, b)) for c in range(a, b, BANK)]


def _lanes(T, topo, rank):
    return len(topo.engines(T.cores[rank], T.cores[rank + 1]))


def R(b, lo, hi, p0=0, p1=128, st=1):
    return ("r", b, lo, hi, p0, p1, st)


def PS(tok, lo, hi, p0=0, p1=128, st=1):
    return ("p", tok, lo, hi, p0, p1, st)


def IX(win, off):
    return ("i", win, off)


def _program(g, T, topo, rank, pace):
    CYC, PCY, GATH, XCH, OV, OA = pace[:6]
    ops, hist, nd, now = [], {}, [0], [0]
    V, A, PE = g.vector, g.scalar, g.tensor

    def op(eng, cost, fn, rd=(), wr=(), tok=None, soft=(), dma=None, lat=0.0, pre=None):
        i = len(ops)
        deps = set()
        for (lst, is_w) in ((rd, False), (wr, True)):
            for r in lst:
                deps |= {j for (j, q, w2) in hist.get(r[1], ()) if (is_w or w2) and q[2] < r[3] and r[2] < q[3] and q[4] < r[5] and r[4] < q[5]}
        for (lst, is_w) in ((rd, False), (wr, True)):
            for r in lst:
                h = hist.setdefault(r[1], [])
                if is_w:
                    h[:] = [e for e in h if not (r[2] <= e[1][2] and e[1][3] <= r[3] and r[4] <= e[1][4] and e[1][5] <= r[5])]
                h.append((i, r, is_w))
        if tok is not None:
            deps |= {j for j in tok["ops"] if ops[j]["e"] != eng}
            soft = list(soft) + tok["ops"][-1:]
            tok["ops"].append(i)
        deps.discard(i)
        ops.append({"e": eng, "c": cost, "fn": fn, "deps": deps, "soft": set(soft) - deps, "tok": tok, "dma": dma, "lat": lat,
                    "pre": pre, "s": now[0]})
        return i

    def token(w):
        return {"ops": [], "b": None, "n": (w + BANK - 1) // BANK}

    def ap(x):
        if not isinstance(x, tuple):
            return x
        if x[0] == "i":
            return ap(x[1]).indirect(ap(x[2]))
        t, c = (T.ps, BANK * x[1]["b"]) if x[0] == "p" else (T[x[1]], 0)
        return t[x[4]:x[5], c + x[2]:c + x[3]:x[6]] if x[6] > 1 else t[x[4]:x[5], c + x[2]:c + x[3]]

    def call(eng, f, fn, out, args, tail=(), kw=None, **k):
        rd, tok = [], None
        for x in list(args) + list((kw or {}).values()):
            if isinstance(x, tuple):
                if x[0] == "p":
                    tok = x[1]
                else:
                    rd += [x] if x[0] == "r" else [x[1], x[2]]
        cost = max(64.0, (out[3] - out[2]) * f) * CYC + (OV if eng == "v" else OA)
        return op(eng, cost, lambda: fn(ap(out), *[ap(x) for x in args], *tail, **{q: ap(x) for q, x in (kw or {}).items()}),
                  rd, [out], tok=tok, **k)

    def ts(out, in0, s1, o0, s2=None, o1=None, f=1.0, **k):
        return call("v", f, V.tensor_scalar, out, [in0, s1, s2], [o0] if o1 is None else [o0, o1], **k)

    def tt(out, in0, in1, o, f=1.0, **k):
        return call("v", f, V.tensor_tensor, out, [in0, in1], [o], **k)

    def act(out, in_, func, f=1.0, soft=(), **kw):
        return call("a", f, A.activation, out, [in_], [func], kw, soft=soft)

    def mset(out, val):
        return call("v", 0.5, V.memset, out, [val])

    def lin(out, in_, scale, bias):
        return act(out, in_, ACT.Identity, scale=scale, bias=bias)

    def fill(out, val):
        return lin(out, R("gcol", 0, out[3] - out[2], out[4], out[5]), 0.0, val)

    def copy(eng, out, in_):
        if eng == "g":
            n = out[3] - out[2]
            return op("g", 200.0 + 2 * CYC * n, lambda: g.affine_select(ap(out), ap(in_), [[0, n]], ALU.is_ge, 0.0, 0, 0), [in_], [out])
        return act(out, in_, ACT.Identity) if eng == "a" else call("v", 1.0, V.tensor_copy, out, [in_])

    def skip(eng, soft=()):
        return op(eng, 0.0, None, soft=soft)

    def mm(groups, start=True, stop=True, **k):
        items = [it for grp in groups for it in grp]
        cost = sum(max(64, (it[0][3] - it[0][2] + it[0][6] - 1) // it[0][6]) for it in items) * PCY + 20.0 + OM * len(items)

        def fn():
            for grp in groups:
                for q, (o, lhs, rhs) in enumerate(grp):
                    last = PE.matmul(ap(o), ap(lhs), ap(rhs), start and q == 0, stop and q == len(grp) - 1)
            return last
        return op("p", cost, fn, [x for it in items for x in it[1:]], (), tok=items[0][0][1], **k)

    def compact(tok, c0, w, src, a, b):
        return [(PS(tok, c0, c0 + (b - a) // 16), R(w, 15 - i, 143 - i), R(src, a + i, b, st=16)) for i in range(16)]

    def summed(a, b, parts, **k):
        tk = token(b - a)
        mm([[(PS(tk, c, c + y - x), whole(m), R(src, c0 + x, c0 + y)) for (m, src, c0) in parts] for (c, x, y) in _banked(a, b)], **k)
        return PS(tk, 0, b - a)

    def iota(out, pattern, base, cm=0):
        kw = {} if out[1] == "pi" else {"allow_small_or_imprecise_dtypes": True}
        return op("g", 160.0 + 2 * CYC * (out[3] - out[2]), lambda: g.iota(ap(out), pattern, base, cm, **kw), (), [out])

    def keep(out, in_, pattern, cmp, base, cm):
        return op("g", 200.0 + 2 * CYC * (out[3] - out[2]), lambda: g.affine_select(ap(out), ap(in_), pattern, cmp, 0.0, base, cm), [in_], [out])

    def dma(eng, out, in_, rd, wr, nbytes, sem=None):
        if sem is None:
            sem = "dm%d" % nd[0]
            nd[0] += 1
        q = g.sync if eng == "s" else g.scalar
        return op(eng, 60.0, lambda: q.dma_start(out, in_), rd, wr, dma=sem, lat=DL + nbytes / BW)

    def col(i, p0=0, p1=128, b="col"):
        return R(b, i, i + 1, p0, p1)

    def whole(b, n=128):
        return R(b, 0, n)

    add, mul, eq, sub = ALU.add, ALU.mult, ALU.is_equal, ALU.subtract
    halves = [(h, 64 * h, 64 * h + 64) for h in range(2)]
    first = [_cuts(x) for x in LOAD]

    dma("a", T.wk[:, 3:6], T.kc[:, :], (), [R("wk", 3, 6)], 0)
    dma("a", T.wk[:, 0:3], T.wa[:, :], (), [R("wk", 0, 3)], 0)
    for k in range(NS):
        for y in range(2):
            dma("a", T.hls[64 + 16 * y:80 + 16 * y, 3 * k:3 * k + 3], T.hl[64 * k:64 * k + 64:4, 3 * y:3 * y + 3], (),
                [R("hls", 3 * k, 3 * k + 3, 64 + 16 * y, 80 + 16 * y)], 0)
    done = 0
    for k in range(NS):
        for (_, a, b) in first[k]:
            for (h, p0, p1) in halves:
                done += (b - a) * 128
                dma("s", T["xw%d0" % k][p0:p1, W0 + a:W0 + b], T.x[64 * k:64 * k + 64, Q * h + a:Q * h + b], (),
                    [R("xw%d0" % k, W0 + a, W0 + b, p0, p1)], done)

    def table(k, done, after, sems, soft=()):
        for (h, p0, p1) in halves:
            i = dma("s", T["tab%d" % k][p0:p1, :], T.inv[64 * k:64 * k + 64, :], after, [R("tab%d" % k, 0, TW, p0, p1)], done + TW * 128 * (h + 1), sems[h])
            ops[i]["soft"] |= set(soft)
    if not ROW:
        table(0, done, (), (None, None))

    iota(R("pi", 0, 1), [[0, 1]], 0, 1)
    iota(R("vs", 0, 64), [[0, 2], [1, 16], [-1, 2]], 0)
    for j in range(4):
        if GEN[0] == "g":
            iota(R("vk", 32 * j, 32 * j + 32), [[1, 16], [-1, 2]], 16 << j)
        else:
            lin(R("vk", 32 * j, 32 * j + 32), R("vs", 0, 32), 1.0, float(16 << j))
    if GEN[1] == "g":
        iota(R("vs", 64, 66), [[0, 2]], -5)
    else:
        lin(R("vs", 64, 66), R("vs", 0, 2), 0.0, -5.0)
    iota(R("gcol", 0, 128), [[2, 2], [4, 4], [0, 16]], 0)
    if GEN[2] == "g":
        iota(R("gcol", 128, 256), [[2, 2], [4, 4], [0, 16]], 1)
    else:
        lin(R("gcol", 128, 256), R("gcol", 0, 128), 1.0, 1.0)
    for j in (3, 2, 1, 0):
        iota(R("pp", 0, 128, 0, 16 * j + 16), [[0, 64 >> j], [4096, 2], [0, 1 << j]], -2048)
    ts(R("pi", 1, 2), R("pi", 0, 1), 15, ALU.bitwise_and)
    ts(R("pi", 2, 3), R("pi", 0, 1), 2, ALU.logical_shift_right, 12, ALU.bitwise_and)
    ts(R("pi", 3, 4), R("pi", 0, 1), 5, ALU.logical_shift_right, 2, ALU.bitwise_and)
    copy("v", R("col", 0, 4), R("pi", 0, 4))
    lin(col(5), col(2), 1.0, col(3))
    for k in range(NS):
        for (h, p0, p1) in halves:
            copy("a", R("cw", 8 * k, 8 * k + 6, p0, p1), R("wk", 0, 6, 64 * k, 64 * k + 64))
        lin(R("ck", 4 * k, 4 * k + 3), R("cw", 8 * k + 3, 8 * k + 6), 16.0, col(5))
    ts(R("as", 0, 66), R("vs", 0, 66), col(5), eq)
    ts(col(7, 64, 96), col(0, 64, 96), 80.0, ALU.is_lt, 0.5, sub)
    lin(col(8, 64, 96), col(7, 64, 96), 14336.0, -5120.0)
    lin(col(9, 64, 96), col(7, 64, 96), -2048.0, 1024.0)
    fill(R("bz", 0, 8, 0, 64), -127.5)
    fill(R("bz", 0, 8, 96, 97), 1.0)
    lin(R("bz", 0, 6, 64, 96), R("hls", 0, 6, 64, 96), -1.0, col(7, 64, 96))
    ts(R("msk", 0, 256, 0, 64), R("gcol", 0, 256, 0, 64), col(1, 0, 64), eq, f=0.5)
    for e in range(2):
        tt(R("fm", 128 * e, 128 * e + 128, 0, 64), R("msk", 128 * e, 128 * e + 128, 0, 64), R("pp", 0, 128, 0, 64), mul)
    copy(GEN[3], R("sm", 0, 256, 0, 64), R("fm", 0, 256, 0, 64))
    ts(R("fm", 0, 256, 64, 96), R("gcol", 0, 256, 64, 96), col(1, 64, 96), eq, col(8, 64, 96), mul, 0.5)
    ts(R("sm", 0, 256, 64, 96), R("gcol", 0, 256, 64, 96), col(1, 64, 96), eq, col(9, 64, 96), mul, 0.5)
    mset(R("fm", 0, 256, 96, 98), 1.0)
    fill(R("fm", 0, 128, 96, 97), 2046.0)
    fill(R("fm", 128, 256, 96, 97), 2048.0)
    mset(R("sm", 0, 256, 96, 97), -8192.0)
    mset(R("ones", 0, RAMP), 1.0)
    call("v", 0.5, V.tensor_tensor_scan, R("ramp", 0, RAMP), [R("ones", 0, RAMP), R("ones", 0, RAMP), -1521.0], [add, add])
    a = RAMP
    while a < Q:
        b = min(2 * a, Q)
        if GEN[5] == "a":
            lin(R("ramp", a, b), R("ramp", 0, b - a), 1.0, 2.0 * a)
        else:
            ts(R("ramp", a, b), R("ramp", 0, b - a), 2.0 * a, add, f=0.5)
        a = b
    for k in range(NS):
        now[0] = k
        if k and ROW:
            row = dma("s", T.tile1[97:98, :], T.tile0[97:98, :], [R("tile0", 0, Q // 2, 97, 98)], [R("tile1", 0, Q // 2, 97, 98)], 0, "row")
            table(0, 0, (), ("ta0", "ta1"), [row])
        else:
            for (_, a, b) in _cuts("768 768"):
                if GEN[6] == "a":
                    lin(R("tile%d" % k, a // 2, b // 2, 96, 98), R("ramp", a, b, 96, 98, 2), 1.0, 1.0)
                else:
                    ts(R("tile%d" % k, a // 2, b // 2, 96, 98), R("ramp", a, b, 96, 98, 2), 1.0, add, f=0.5)
        lin(R("dd%d" % k, 0, 1), col(1), 2.0, 32.0 - 1584.0)
    now[0] = 0
    for (h, p0, p1) in halves[::-1]:
        iota(R("tag", 0, 1, 0, p1), [[0, 1]], 1024 * (2 * rank + 1 + h))
    em = R("em", 0, 144)
    keep(whole("id1"), whole("ones"), [[-1, 128]], eq, 0, 1)
    keep(em, R("ones", 0, 144), [[0, 9], [1, 16]], eq, -15, 0)
    keep(em, em, [[-1, 144]], ALU.is_ge, 15, 1)
    keep(em, em, [[1, 144]], ALU.is_ge, 0, -1)
    ts(R("q16", 0, 16), R("vs", 0, 32, st=2), col(1), ALU.is_lt, 1.0, add)
    call("v", 1.0, V.tensor_reduce, col(11), [R("q16", 0, 16)], [AX.X, mul])
    ts(col(12), col(1), 12.0, ALU.is_lt, 1.0 / 256, mul)
    ts(R("pf", 0, 144), R("em", 0, 144), col(11), mul, col(12), mul, 0.5)
    if not LCPRE:
        lin(R("pl", 0, 144), R("pf", 0, 144), -128.0, 0.0)
    for (e, v) in (("a", 256.0), ("v", 512.0)):
        if e in CUT["low"] + LAST.get("low", "") + FIRST.get("low", ""):
            if GEN[4] == "a":
                lin(whole("id" + e), whole("id1"), v, 0.0)
            else:
                iota(whole("id" + e), [[0, 128]], int(v))
                keep(whole("id" + e), whole("id" + e), [[-1, 128]], eq, 0, 1)
    for (e, v) in (("a", -1600), ("v", 100352)):
        mine = [c for c in _cuts(CUT["sel"]) if c[0] == e]
        if mine:
            iota(R("kz", mine[0][1] // 16, mine[-1][2] // 16), [[0, (mine[-1][2] - mine[0][1]) // 16]], v)

    def setup(k, u):
        n = "%d%d" % (k, u)
        ts(R("lt" + n, 0, 128), whole("vk"), col(4 * k + u, b="ck"), eq, f=0.5)
        lin(R("lt" + n, 128, 194), R("as", 0, 66), col(8 * k + u, b="cw"), 0.0)
        if u > 0 and EARLY < Q:
            tk = token(1)
            mm([[(PS(tk, 0, 1, 0, 97), R("lt" + n, e, 194, st=2), R("ones", 0, 1)) for e in range(2)]])
            lin(col(3 * k + u + 8, 0, 97, "bz"), PS(tk, 0, 1, 0, 97), KN, col(3 * k + u, 0, 97, "bz"))
        if FOLD:
            iota(R("cb" + n, 0, 16), [[0, 16]], int(NC))
        iota(R("xw" + n, 0, 32), [[-16384, 2], [0, 16]], int(NC))
        iota(R("land" + n, 48, 64, 0, 64), [[0, 16]], int(NC))

    def rule(k, u):
        n, z = "%d%d" % (k, u), NS * u + k
        cut = {x: _cuts({0: FIRST, RU - 1: LAST}.get(u, {}).get(x, y)) for x, y in CUT.items()}
        xw, tile, dd = "xw" + n, "tile%d" % k, "dd%d" % k
        lo, fb, nb, yo, got, sel, rr, ss, bb, tab, offi, offc, ia, ib, mx, lc = [
            "%s%d" % (x, k) for x in "lo fb nb yo got sel rr ss bb tab offi offc ia ib mx lc".split()]
        window = R(xw, 0, W0 + Q)

        def form(tk, w, rows, c, x, y):
            return [(PS(tk, c + e, c + y - x, st=2), R(w, 128 * e, 128 * e + 128, 0, rows), R(tile, x // 2, y // 2, 0, rows)) for e in range(2)]
        for (_, a, b) in cut["sign"]:
            w = (b - a) // 2
            tk = token(w)
            early = u > 0 and a >= EARLY
            parts = [(ss, 0), (nb, 0)] if early else [(xw, W0)]
            mm([[(PS(tk, c, c + y - x, 0, 97), R("lt" + n, e, 194, st=2), R(src, c0 + 2 * x + e, c0 + 2 * y, st=2)) for (src, c0) in parts for e in range(2)]
                for (c, x, y) in _banked(a // 2, b // 2)])
            act(R(tile, a // 2, b // 2, 0, 97), PS(tk, 0, w, 0, 97), ACT.Sign, bias=col(3 * k + u + 8 * early, 0, 97, "bz"))
        for (_, a, b) in cut["scan"]:
            tk = token(b - a)
            mm([[m] for run in _banked(a, b) for m in form(tk, "fm", 98, *run)])
            call("v", 1.0, V.tensor_tensor_scan, R(dd, a + 1, b + 1), [PS(tk, 0, b - a), R("ramp", a, b), R(dd, a, a + 1)], [ALU.max, ALU.min])
        end, even, half = R(dd, Q, Q + 1), R(mx, 64, 65), R(mx, 68, 69)
        ts(even, end, EVEN, add, EVEN, sub)
        lin(half, end, 0.5, 792.0)
        ts(R(offi, 96, 97), end, even, eq, half, mul)
        for (e, a, b) in cut["sel"]:
            tk = token(b - a)
            if e == "a":
                mm([[(PS(tk, c, c + y - x), whole("id1"), R(dd, x, y))] + form(tk, "sm", 97, c, x, y) for (c, x, y) in _banked(a, b)])
                act(R(sel, a, b), PS(tk, 0, b - a), ACT.Relu, bias=-448.0)
            else:
                mm([[m] for run in _banked(a, b) for m in form(tk, "sm", 97, *run)], soft=[h[0] for h in hist[dd] if h[2] and h[1][2] <= a < h[1][3]])
                tt(R(sel, a, b), R(dd, a, b), PS(tk, 0, b - a), ALU.min)
        for (_, a, b) in cut["find"]:
            ka, kb = a // 16, b // 16
            tk = token(kb - ka)
            mm([[(PS(tk, 0, kb - ka), whole("id1"), R("kz", ka, kb))] + compact(tk, 0, "em", sel, a, b)])
            ts(R(ia, ka, kb), PS(tk, 0, kb - ka), 2047.5, mul, 808.25, add)
            ts(R(ib, ka, kb), R(ia, ka, kb), 4095, ALU.bitwise_and)
            found = ts(R(offi, ka, kb), R(ib, ka, kb), -1.0, mul, 1600.0, add)
        sm, cb, land = "sm" + n, "cb" + n, "land" + n
        if LOC[2] == "a":
            sent = lin(R(sm, 0, 16), IX(window, R(offi, 96, 97)), 1.0, col(0, b="tag"))
        else:
            sent = ts(R(sm, 0, 16), IX(window, R(offi, 96, 97)), col(0, b="tag"), add)
        copy(LOC[0], R(land, 48, 64, 64, 128), R(sm, 0, 16, 0, 64))
        dsts = [rank + d for d in range(1, HB + 1) if rank + d < len(T.cores)]
        srcs = [R(sm, 0, 16), R(cb, 0, 16), R(land, 48, 64)] if FOLD else [R(cb, 0, 16)]
        if not dsts:
            for e in (LOC[1] if FOLD else "v" + LOC[1]):
                skip(e)
        elif FOLD:
            copy(LOC[1], R(cb, 0, 16, 0, 64), R(sm, 0, 16, 64, 128))
        else:
            tt(R(cb, 0, 16, 64, 128), R(sm, 0, 16, 64, 128), R(land, 48, 64, 64, 128), ALU.max)
            copy(LOC[1], R(cb, 0, 16, 0, 64), R(cb, 0, 16, 64, 128))

        def send():
            ids = [DstId(rid=topo.addr(T.cores[r2])[0], pnc=topo.addr(T.cores[r2])[1]) for r2 in dsts]
            g.remote_dma_fused([RemoteDMATransfer(dst_ids=ids, dma_engine_mask=topo.mask(T.cores[rank], T.cores[dsts[0]]), remote_sem=T.sem["arr%d" % z],
                                                  srcs=[ap(x) for x in srcs], dsts=[ap(R(land, 16 * q, 16 * q + 16)) for q in range(len(dsts))],
                                                  alu_op=2 if FOLD else 0)], local_sem=T.sem.loc)
        sent = op("g", 1000.0, send if dsts else None, srcs if dsts else (), (), soft=[sent], lat=XCH - 1000.0 + FOLD * FX)

        def bound(a, b, **k2):
            e = [c[0] for c in cut["low"] if c[1] <= a < c[2]][0]
            return summed(a, b, [("id1", xw, W0), ("id" + e, lo, 0)], **k2)
        runs = []
        for (e, a, b) in cut["low"]:
            if e == "a":
                act(R(lo, a, b), R(xw, W0 + a, W0 + b), ACT.Sign, bias=-63.5)
            else:
                ts(R(lo, a, b), R(xw, W0 + a, W0 + b), 64.0, ALU.is_ge, 0.5, sub, 0.5)
            if runs and runs[-1][0] == e:
                runs[-1][2] = b
            else:
                runs.append([e, a, b])
        for (e, a, b) in cut["copy"]:
            if e == "v":
                copy("a", R(bb, a, b), bound(a, b))
        for (e, a, b) in (runs if LCPRE else []):
            tk = token((b - a) // 16)
            mm([compact(tk, 0, "pf", lo, a, b)])
            lin(R(lc, a // 16, b // 16), PS(tk, 0, (b - a) // 16), -128.0 if e == "a" else -256.0, 0.5)
        ns = min(rank, HB)
        pre, src = (("arr%d" % z, sum(_lanes(T, topo, rank - q) for q in range(1, ns + 1))) if ns else None), R(land, 48, 64)
        if ns == 3:
            tt(R(mx, 0, 32), R(land, 0, 32), R(land, 32, 64), ALU.max, soft=[sent], pre=pre)
            tt(R(mx, 32, 48), R(mx, 0, 16), R(mx, 16, 32), ALU.max)
            src = R(mx, 32, 48)
        else:
            for q in range(ns):
                tt(R(mx, 16 * q, 16 * q + 16), R(land, 16 * q, 16 * q + 16), src, ALU.max, soft=[sent], pre=pre)
                src, pre = R(mx, 16 * q, 16 * q + 16), None
            for q in range(ns, 2):
                skip("v")
        ts(R(mx, 48, 64), src, MAGIC, add, MAGIC, sub, soft=[sent])
        tt(R(xw, 16, 32), src, R(mx, 48, 64), sub)
        for (e, a, b) in cut["copy"]:
            src = IX(window, R(offi, a // 16, b // 16))
            if e == "a":
                act(R(got, a, b), src, ACT.Identity, GATH)
                tt(R(rr, a, b), R(got, a, b), bound(a, b, soft=[found]), ALU.max)
            else:
                tt(R(rr, a, b), src, R(bb, a, b), ALU.max, GATH)
        if z == 0:
            table(1, 0, [R(rr, 0, 16)], ("tb0", "tb1"))
        for (_, a, b) in cut["bits"]:
            ts(R(fb, a, b), R(rr, a, b), 0.0, ALU.max, KF - 63.5, add, 0.5)
        for (_, a, b) in cut["code"]:
            ka, kb = a // 16, b // 16
            tk = token(kb - ka)
            if LCPRE:
                mm([[(PS(tk, 0, kb - ka), whole("id1"), R(lc, ka, kb))] + compact(tk, 0, "pf", fb, a, b)])
            else:
                mm([compact(tk, 0, "pl", lo, a, b)], stop=False, soft=[h[0] for h in hist[rr] if h[2] and h[1][2] <= a < h[1][3]])
                mm([compact(tk, 0, "pf", fb, a, b)], start=False)
            ts(R(offc, ka, kb), PS(tk, 0, kb - ka), 2.0, mul, -(KF / 128 + 1) * 4095 - LCPRE, add)
        for j, (e, a, b) in enumerate(cut["sum"]):
            src = IX(R(tab, 0, TW), R(offc, a // 16, b // 16))
            if e == "a":
                act(R(ss, a, b), src, ACT.Identity, GATH)
            else:
                tt(R(ss, a, b), src, R(rr, a, b), add, GATH)

        def terms(a):
            return [("id1", ss, 0)] + [("id1", rr, 0) for c in cut["sum"] if c[0] == "a" and c[1] <= a < c[2]]
        for (e, a, b) in cut["floor"]:
            two = len(terms(a)) == 2
            src = summed(a, b, terms(a)) if two else R(ss, a, b)
            if e == "a":
                lin(R(nb, a, b), src, -1.0, 127.5 - KN)
            else:
                ts(R(nb, a, b), src, -1.0, mul, 127.5 - KN, add, 1.0 if two else 0.5)
        nx, no = (yo, 0) if u == RU - 1 else ("xw%d%d" % (k, u + 1), W0)
        for (e, a, b) in cut["out"]:
            src = summed(a, b, terms(a) + [("id1", nb, 0)])
            if e == "v":
                ts(R(nx, no + a, no + b), src, KN, add)
            else:
                lin(R(nx, no + a, no + b), src, 1.0, KN)
            if u == RU - 1:
                for (h, p0, p1) in halves:
                    dma("s", T.y[64 * k:64 * k + 64, Q * h + a:Q * h + b], T[nx][p0:p1, a:b], [R(nx, a, b, p0, p1)], (), (b - a) * 256, sem="st")

    for stage in (setup, rule):
        for u in range(RU):
            for k in range(NS):
                now[0] = k
                stage(k, u)
    return ops


def _graph(ops, pace):
    pred = [sorted(o["deps"] | o["soft"]) for o in ops]
    succ, gap = [[] for _ in ops], {}
    for i, o in enumerate(ops):
        for d in pred[i]:
            succ[d].append(i)
            gap[d, i] = ops[d]["lat"] + (pace[6] if ops[d]["e"] != o["e"] or ops[d]["dma"] else pace[7] * (d in o["deps"]))
    return pred, succ, gap, pace[6]


def _place(ops, graph, key, back):
    pred, succ, gap = graph[:3]
    up, down = (succ, pred) if back else (pred, succ)
    left = [len(x) for x in up]
    ready = [i for i in range(len(ops)) if not left[i]]
    at, taken = [0.0] * len(ops), {e: [] for e in "vapgs"}
    while ready:
        i = min(ready, key=lambda j: key[j])
        ready.remove(i)
        c, row = ops[i]["c"], taken[ops[i]["e"]]
        t = max([ops[i]["lat"] if back else 0.0] + [at[d] + ops[d]["c"] + (gap[i, d] if back else gap[d, i]) for d in up[i]])
        k = len(row)
        while k and row[k - 1][1] > t:
            k -= 1
        while k < len(row) and row[k][0] < t + c:
            t = max(t, row[k][1])
            k += 1
        row.insert(k, (t, t + c))
        at[i] = t
        for j in down[i]:
            left[j] -= 1
            if not left[j]:
                ready.append(j)
    return at


def _banks(ops, graph, at):
    pred, _, gap, hop = graph
    todo = sorted(range(len(ops)), key=lambda i: (at[i], i))
    fin, free, held, order, start, bank = {}, {}, [None] * 8, [], [0.0] * len(ops), {}
    while todo:
        for x, i in enumerate(todo):
            if not all(d in fin for d in pred[i]):
                continue
            tok = ops[i]["tok"]
            if tok is None or tok["ops"][0] != i:
                tok = None
                break
            since = [0.0 if not k else max(fin[j] for j in k["ops"]) if all(j in fin for j in k["ops"]) else None for k in held]
            spare = [(max(since[b:b + tok["n"]]), b) for b in range(0, 9 - tok["n"], tok["n"]) if None not in since[b:b + tok["n"]]]
            if spare:
                break
        todo.pop(x)
        o = ops[i]
        t = max([free.get(o["e"], 0.0)] + [fin[d] + gap[d, i] for d in pred[i]])
        if tok is not None:
            f, b = min(spare)
            bank[i] = (b, {j for k in held[b:b + tok["n"]] if k for j in k["ops"] if ops[j]["e"] != "p"})
            held[b:b + tok["n"]], t = [tok] * tok["n"], max(t, f + hop)
        start[i], free[o["e"]] = t, t + o["c"]
        fin[i] = t + o["c"]
        order.append(i)
    return max(fin[i] + ops[i]["lat"] for i in fin), order, start, bank


def _replay(ops, graph, order, bank):
    pred, _, gap, hop = graph
    fin, free = [0.0] * len(ops), {e: 0.0 for e in "vapgs"}
    for i in order:
        t = max([free[ops[i]["e"]]] + [fin[d] + gap[d, i] for d in pred[i]] + [fin[d] + hop for d in (bank[i][1] if i in bank else ())])
        free[ops[i]["e"]] = fin[i] = t + ops[i]["c"]
    return max(fin[i] + ops[i]["lat"] for i in order)


def _plan(progs, rounds):
    ops, graphs = progs[0], [_graph(p, pace) for p, pace in zip(progs, PACES)]
    n, graph, rng = len(ops), graphs[0], np.random.default_rng(SEED)
    loads = [i for i in range(n) if (ops[i]["dma"] or "").startswith("dm")]

    def tighten(key, passes=(False, True, False), limit=1e9):
        for back in passes:
            for i in ([] if back else loads):
                key[i] = i - 1e9
            at = _place(ops, graph, key, back)
            key = [-(at[i] + ops[i]["c"]) for i in range(n)]
        end, order, start, bank = _banks(ops, graph, at)
        if end > limit:
            return (1e9,)
        ends = [end] + [_replay(p, q, order, bank) for p, q in zip(progs[1:], graphs[1:])]
        return sum(e * PACES[0][0] / pace[0] for e, pace in zip(ends, PACES)) / len(PACES), ends, start
    rest, stream = [0.0] * n, np.array([o["s"] for o in ops])
    for i in range(n - 1, -1, -1):
        rest[i] = ops[i]["c"] + max([ops[i]["lat"]] + [graph[2][i, j] + rest[j] for j in graph[1][i]])
    best = now = tighten([-rest[i] - (LEAD if ops[i]["s"] == 0 else 0.0) for i in range(n)])
    for r in range(rounds):
        at = np.array(now[2])
        near = abs(at - rng.random() * at.max()) < rng.choice([1500.0, 3000.0, 6000.0])
        if rng.random() < 0.3:
            shake = rng.normal(0.0, 1500.0) * (stream == rng.integers(NS))
        else:
            shake = rng.normal(0.0, rng.choice([200.0, 500.0, 1200.0]), n) * (rng.random(n) < 0.5)
        new = tighten([float(t) for t in at + shake * near], (False, True, False)[:rng.choice([1, 3])], now[1][0] + 400.0)
        if new[0] < now[0] - 15.0 * (1 - r / rounds) * np.log(rng.random()):
            now = new
        if new[0] < best[0]:
            best = new
    return best


PLAN = {}


def _arrange(ops, at):
    end, order, start, bank = _banks(ops, _graph(ops, PACES[0]), at)
    for i, (b, waits) in bank.items():
        ops[i]["tok"]["b"] = b
        ops[i]["deps"] |= waits
    return order, end, start


def rank_program(g, core, T, topo):
    rank = T.rank_of(core)
    if rank is None:
        return
    ops = _program(g, T, topo, rank, PACES[0])
    if not PLAN:
        PLAN["at"] = _plan([_program(g, T, topo, HB, pace) for pace in PACES], ROUNDS)[2]
    order = _arrange(ops, PLAN["at"])[0]
    queue = {"v": g.vector, "a": g.scalar, "p": g.tensor, "g": g, "s": g.sync}
    needed = set().union(*[o["deps"] for o in ops])
    mark, total, clock, known = {}, {}, {}, {e: {} for e in queue}
    place = {i: p for p, i in enumerate(order)}
    for i in order:
        o = ops[i]
        if o["fn"] is None:
            continue
        q, kn = queue[o["e"]], known[o["e"]]
        for d in sorted(o["deps"], key=lambda d: -place[d]):
            s, v = mark[d]
            if kn.get(s, 0) < v:
                q.wait_ge(T.sem[s], v)
                kn[s] = v
                for s2, v2 in clock[d].items():
                    kn[s2] = max(kn.get(s2, 0), v2)
        if o["pre"] is not None:
            q.wait_ge(T.sem[o["pre"][0]], o["pre"][1])
        ins = o["fn"]()
        if o["dma"] or i in needed:
            s = o["dma"] or ENGSEM[o["e"]]
            total[s] = total.get(s, 0) + (16 if o["dma"] else 1)
            mark[i], clock[i] = (s, total[s]), dict(kn)
            ins.then_inc(T.sem[s], 16 if o["dma"] else 1)
    if rank + 1 < len(T.cores):
        g.wait_ge(T.sem.loc, RU * NS * _lanes(T, topo, rank))
    for s in sorted(total, key=lambda s: s == "st"):
        g.wait_ge(T.sem[s], total[s])
